import numpy as np, ml_dtypes
CORES = [13,21,141,149]
N = 4
BF = ml_dtypes.bfloat16
P, CAP, J, W, D, RO = 512, 128, 8, 4096, 3, 8
WT = np.array([1, 3, 7, 13, 21, 35, 49, 67, 85, 107, 129, 155, 181, 211, 241, 253], np.int32)
KA = np.array([17, 101, 263, 389, 547, 701, 859, 1021], np.int32)
def mark(s):
    return np.add.reduce(s * WT[:, None], axis=-2) & 4095
def columns(u, e):
    return ((u * u >> 4)[..., None, :] + KA[:, None] * u[..., None, :] + 811 * e) & (W - 1)
def lanes(rng, v, k):
    return np.minimum((rng.random((N, 8, 16, k), dtype=np.float32) * (v + 1)[:, None, None]).astype(np.int32), v[:, None, None])
def toward(s, r):
    z = np.array(s); z[0] = (s[0] & (64 - N)) + ((s[0] + r - mark(s)) & (N - 1))
    return z
def pack(o, s, c):
    return {"opr": np.ascontiguousarray(o.reshape(N, 128, W)).astype(np.float32).astype(BF), "s0": np.ascontiguousarray(s.reshape(N, 128, P)).astype(np.float32).astype(BF),
            "f0": np.ascontiguousarray(c).astype(np.int32)}
def setup_inputs(rng):
    t = rng.permutation(8); v = np.full(8, 63); v[t[0]] = rng.choice(np.array([1, 3])); v[t[1]] = 15
    span = rng.choice(np.array([40, 100, 200, 400]), (8, 1)); span[t[0]] = 1
    c = (rng.random((N, 8, P)) * (span + 1)).astype(np.int64)
    c = np.where(rng.random((N, 8, P)) < rng.choice(np.array([0.0, 0.1, 0.3]), (N, 8, 1)), 1023, c)
    return pack(lanes(rng, v, W), lanes(rng, v, P), c)
def setup_inputs_spread(rng):
    o = np.minimum((np.exp2(6 * rng.random((N, 8, 1, W))) * rng.random((N, 8, 16, W))).astype(np.int64), 63)
    s = np.minimum((np.exp2(6 * rng.random((N, 8, 1, P))) * rng.random((N, 8, 16, P))).astype(np.int64), 63)
    c = np.minimum(np.exp2(10 * rng.random((N, 8, P))).astype(np.int64) - 1, 1022)
    return pack(o, s, np.where(rng.random((N, 8, P)) < 0.125, 1023, c))
def setup_inputs_ends(rng):
    o = 63 * rng.integers(0, 2, (N, 8, 16, W)); s = 63 * rng.integers(0, 2, (N, 8, 16, P))
    share = rng.permutation(np.array([1.0, 1.0, 1.0, 0.9, 0.7, 0.5, 0.3, 0.1]))
    c = np.where(rng.random((N, 8, P)) < share[:, None], 0, 1023)
    m = 63 * ((np.arange(65536)[:, None] >> np.arange(16)) & 1)
    u = np.arange(4096); free = np.zeros((4096, 16), np.int64)
    free[:, 15] = u // 253; free[:, 4] = (u % 253) // 21; free[:, 0] = (u % 253) % 21
    every = columns(mark(free.T), 0)
    for k, x in ((P - 3, int(np.max(every))), (P // 2, int(np.min(every)))):
        for b in (m, free):
            z = np.nonzero(np.any(columns(mark(b.T), 0) == x, axis=0))[0]
            if len(z):
                s[:, :, :, k] = b[rng.choice(z, (N, 8))]; c[:, :, k] = 0
                break
    s[..., [0, 1, P - 2, P - 1]] = 63; c[..., [0, P - 1]] = 0; c[..., [1, P - 2]] = 1023
    a = columns(mark(np.full((16, 1), 63)), 0)[:, 0]
    o[..., a[0]] = 0; o[..., a[J - 1]] = 63
    return pack(o, s, c)
def setup_inputs_corners(rng):
    t = rng.permutation(8); v = np.full(8, 63); v[t[6]] = 1; v[t[7]] = 7
    o = lanes(rng, v, W); s = lanes(rng, v, P); c = np.full((N, 8, P), 1023); n = CAP // J; big = int(rng.integers(0, N))
    o[:, t[7]] = 0; c[:, t[0]] = 0; c[N - 1, t[2], P - 1] = 0
    c[:, t[6]] = rng.integers(1012, 1024, (N, P)); c[:, t[7]] = rng.integers(0, 101, (N, P))
    a = columns(mark(np.full((16, 1), 63)), 0)[:, 0]
    for q in range(N):
        for k in (3, 4, 5):
            g = int(t[k]); x = rng.integers(0, 16, 16); x[0] = 0
            x[0] = (q + 1 - int(mark(x[:, None])[0])) & (N - 1)
            o[q, g][:, a] = (63 - x)[:, None]; b = 300 - (int(np.add.reduce(x)) >> 2)
            if k == 5: c[q, g] = np.where(rng.random(P) < 0.5, rng.integers(400, 700, P), 1023)
            w = n + k - 3 if k < 5 else n + 1 if q == big else int(rng.integers(0, n + 1))
            p = np.append(P - 1, rng.permutation(P - 1))[:w]
            s[q, g][:, p] = 63; c[q, g, p] = b
            if k == 4: c[q, g, p[-1]] = b + 1
    return pack(o, s, c)
def setup_inputs_edges(rng):
    t = [int(k) for k in rng.permutation(8)]; v = np.full(8, 63); v[t[7]] = 15
    n = CAP // J; r = int(rng.integers(0, N)); big = int(rng.integers(0, N)); top = int(rng.integers(520, 1001))
    o = lanes(rng, v, W); s = lanes(rng, v, P)
    c = (rng.random((N, 8, P)) * rng.choice(np.array([41, 101, 201]), (8, 1))).astype(np.int64)
    c = np.where(rng.random((N, 8, P)) < 0.1, 1023, c)
    o[:, t[:3]] = 0; c[:, t[0]] = rng.integers(1, 201, (N, P)); c[:, t[1:5]] = 1023
    for q in range(N):
        for k in range(3):
            w = n if k == 1 else n + (k == 0) if q == big else int(rng.integers(0, n + 1))
            p = np.append(P - 1, rng.permutation(P - 1))[:w]
            z = toward(s[q, t[k]][:, p], r)
            if k == 0: z = 0 * z
            s[q, t[k]][:, p] = z; h = np.add.reduce(z, axis=0) >> 2
            if k == 0: c[q, t[k], p] = 0
            elif k == 1: c[q, t[k], p] = top + np.arange(q * n, q * n + n) * 8 // (N * n) - 2 * h
            else: c[q, t[k], p] = 1022 - 2 * h
    for k in (3, 4):
        x = t[k]; z = rng.integers(1, 8, 16); z[0] += (2 - int(mark(z[:, None])[0])) & 3
        h = int(np.add.reduce(z)) >> 2; o[:, x] = rng.integers(56, 64, (N, 16, W))
        for e in range(D): o[:, x, :, int(columns(mark(z[:, None]), e)[0, 0])] = 0
        q = rng.permutation(N); a = int(q[0]); p = np.append(P - 1, rng.permutation(P - 1))[:CAP + 1]
        if k == 3: b = int(q[1]); low = 1022 - 3 * h; more = 1
        else: b = a; low = int(rng.integers(850, 911)); more = h
        s[a, x][:, p[1:]] = z[:, None]; c[a, x, p[1:]] = low + more
        s[b, x, :, P - 1] = z; c[b, x, P - 1] = low
    return pack(o, s, c)
def setup_inputs_ties(rng):
    v = rng.permutation(np.array([1, 1, 3, 3, 7, 15, 31, 63])); o = lanes(rng, v, W); s = lanes(rng, v, P)
    c = rng.choice(np.array([0, 5, 9]), (1, 8, 1)) + rng.integers(0, 2, (N, 8, P)) * rng.choice(np.array([0, 1, 3]), (1, 8, 1))
    s[:, 1::2, :, P // 2:] = s[:, 1::2, :, :P // 2]
    c = np.where(rng.random((N, 8, P)) < 0.05, 1023, c)
    x = int(np.nonzero(v == 1)[0][0]); y = int(np.nonzero(v == 3)[0][0])
    o[:, x] = 0; c[:, x] = 1023
    s[:, x] = rng.integers(0, 64, (N, 16, P)); s[:, x, 0] = np.maximum(s[:, x, 0], 4)
    for q in range(N):
        p = np.append(P - 1, rng.permutation(P - 1))[:CAP // J]
        a = np.add.reduce(s[q, x][:, p], axis=0) >> 2
        c[q, x, p] = 1022 - a - rng.integers(0, a)
    z = rng.integers(1, 8, 16); z[0] += (2 - int(mark(z[:, None])[0])) & 3
    a = int(np.add.reduce(z)) >> 2; b = int(rng.integers(850, 931))
    o[:, y] = rng.integers(56, 64, (N, 16, W)); c[:, y] = 1023
    for e in range(D): o[:, y, :, int(columns(mark(z[:, None]), e)[0, 0])] = 0
    q = rng.permutation(N); p = rng.permutation(P)[:CAP]
    s[int(q[0]), y][:, p] = z[:, None]; c[int(q[0]), y, p] = b + a
    s[int(q[1]), y, :, P - 1] = z; c[int(q[1]), y, P - 1] = b
    return pack(o, s, c)
def check_inputs(d):
    bad = []
    for k, lo, hi in (("opr", 0, 63), ("s0", 0, 63), ("f0", 0, 1023)):
        x = np.asarray(d[k]).astype(np.float64)
        if not (np.min(x) >= lo and np.max(x) <= hi): bad.append("range of " + k)
        elif np.any(x != np.floor(x)): bad.append("whole numbers of " + k)
    return bad
def reference(opr, s0, f0):
    o = opr.astype(np.float32).astype(np.int32).reshape(N, 8, 16, W); gi = np.arange(8)
    S = np.zeros((N, 8, D + 1, 16, P), np.int32); F = np.full((N, 8, D + 1, P), 1023, np.int32)
    S[:, :, 0] = s0.astype(np.float32).astype(np.int32).reshape(N, 8, 16, P); F[:, :, 0] = f0
    lo = np.zeros((8, D), np.int32); hi = np.zeros((8, D), np.int32); U = np.full(8, 1023, np.int32); lev = np.zeros(8, np.int32)
    for rnd in range(RO):
        s = S[:, gi, lev]; f = F[:, gi, lev]; low = lo[gi, lev][:, None]
        h = columns(mark(s), lev[:, None, None]).reshape(N, 8, 1, J * P)
        c = np.abs(np.tile(s, (1, 1, 1, J)) - np.take_along_axis(o, h.astype(np.int64), axis=3))
        fc = np.tile(f, (1, 1, J)) + (np.add.reduce(c, axis=2) >> 2); own = mark(c) & (N - 1)
        B = np.full(8, 1023, np.int32)
        for a in range(N):
            x = np.partition(np.where((fc >= low) & (own == a), fc, 4000), CAP, axis=2)[:, :, CAP]
            B = np.minimum(B, np.min(x, axis=0))
        keep = (fc >= low) & (fc < B[:, None])
        m = np.min(np.where(keep, fc, 4000), axis=(0, 2))
        ns = np.zeros((N, 8, 16, P), np.int32); nf = np.full((N, 8, P), 1023, np.int32)
        for a in range(N):
            k = keep & (own == a); place = np.add.accumulate(k, axis=2, dtype=np.int64) - 1
            qi, ji, ci = np.nonzero(k); t = qi * CAP + place[qi, ji, ci]
            ns[a, ji, :, t] = c[qi, ji, :, ci]; nf[a, ji, t] = fc[qi, ji, ci]
        S[:, gi, lev + 1] = ns; F[:, gi, lev + 1] = nf; hi[gi, lev] = B
        U = np.where(lev == D - 1, np.minimum(U, m), U)
        for g in range(8):
            e = int(lev[g])
            if e == D - 1 or m[g] >= U[g]:
                lo[g, e] = max(int(B[g]), int(lo[g, e]) + 1)
                if lo[g, e] >= U[g] and e > 0:
                    lo[g, e] = 0; e -= 1; lo[g, e] = max(int(hi[g, e]), int(lo[g, e]) + 1)
            else:
                e += 1; lo[g, e] = 0
            lev[g] = e
    yl = np.ascontiguousarray(S[:, :, 1:].transpose(0, 1, 3, 2, 4)).reshape(N, 128, D * P)
    yt = np.concatenate([lo, hi, lev[:, None], U[:, None]], axis=1)
    return {"yl": yl.astype(np.float32).astype(BF), "yf": np.ascontiguousarray(F[:, :, 1:]).reshape(N, 8, D * P).astype(np.float32), "yt": np.stack([yt] * N).astype(np.float32)}

@@ -1,0 +1,658 @@
+from concourse.bass import DstId, RemoteDMATransfer
+from concourse.mybir import AluOpType as O, AxisListType, ActivationFunctionType as F
+
+NR = 8
+SL = 576
+EMPTY = 9
+WT = [1, 3, 7, 13, 21, 35, 49, 67, 85, 107, 129, 155, 181, 211, 241, 253]
+KA = [17, 101, 263, 389, 547, 701, 859, 1021]
+MAGIC = float(3 << 22)
+
+_f, _b, _h, _i, _u = "float32", "bfloat16", "float16", "int32", "uint16"
+PSUM = ("PU", "PX", "PN", "PC0", "PC1", "PEA", "PEB", "PL")
+SCRATCH = {}
+for _n, _w, _d in (
+        ("A", 10 * SL, _b), ("OPW", 4096, _b), ("SND", NR * SL, _b), ("MB", NR * 16, _f), ("S", 512, _b), ("FS", 128, _b), ("D", 4096, _b),
+        ("GA", 1024, _b), ("CH", 4112, _b), ("OFA", 40, _u), ("OFO", 256, _u), ("OFB", 32, _u), ("OFW", 32, _u), ("OFV", 16, _u),
+        ("OFC", 32, _u), ("OFN", 32, _u), ("UI", 32, _i), ("UU", 32, _i), ("UF", 32, _f), ("USQ", 32, _i), ("BB", 32, _i),
+        ("TJ", 256, _f), ("VJ", 256, _i), ("VK", 256, _i), ("XI", 256, _i), ("Y", 256, _i), ("OW", 256, _i), ("OW3", 256, _f), ("OW4", 256, _f),
+        ("Z", 256, _f), ("YW", 272, _f), ("X", 768, _f), ("XH", 512, _h), ("DA", 512, _b), ("DV", 512, _b), ("KP", 1024, _b), ("R", 1024, _b),
+        ("W", 1088, _b), ("IA", 1536, _b), ("IB", 512, _b), ("OH", 1536, _b), ("CG", 1536, _h), ("EBW", 128, _b), ("AB", 96, _b), ("CB", 32, _b),
+        ("EM", 96, _f), ("EA", 12, _f), ("T8", 64, _f), ("P8", 64, _f), ("TT", 4, _f), ("TTH", 4, _f), ("TU", 4, _f), ("CN", 4, _f),
+        ("SV", 64, _f), ("SW", 64, _f), ("MD", 16, _f),
+        ("ONE", 256, _b), ("ZERO", 256, _b), ("BLK", 128, _b), ("BLKF", 128, _f), ("NUT", 128, _b), ("ID", 128, _b), ("IDN", 128, _b),
+        ("IDF", 128, _b), ("ID16", 128, _b), ("S1", 144, _b), ("SD", 144, _b), ("SE", 144, _b), ("S32", 144, _h), ("WM", 144, _b), ("XB", 144, _h),
+        ("K", 512, _b), ("K1", 512, _b), ("CL", 40, _f), ("O32", 32, _b), ("O272", 32, _b), ("DM", 64, _f), ("LM", 16, _f), ("WR", 16, _f),
+        ("W2", 16, _f), ("LC", 16, _f), ("LI", 8, _i), ("BO", 4, _f), ("E8C", 4, _f), ("G8", 8, _h), ("G8F", 8, _f),
+        ("S3", 3072, _b), ("FF", 384, _b), ("F3", 96, _f), ("KP3", 96, _b), ("R3", 96, _b), ("RM", 96, _b), ("W3", 96, _b),
+        ("OF3", 96, _u), ("OG3", 120, _u), ("OP3", 96, _u), ("B8C", 96, _b), ("B256", 96, _b), ("DM3", 96, _f), ("YL", 1536, _b), ("YT", 8, _f)):
+    SCRATCH[_n] = ("sbuf", [128, _w], _d)
+for _n, _w, _d in (("B8", 144, _h), ("F8I", 512, _i), ("F8", 512, _h), ("YF", 1536, _f), ("YT8", 8, _f)):
+    SCRATCH[_n] = ("sbuf", [8, _w], _d)
+for _n in PSUM:
+    SCRATCH[_n] = ("psum", [128, 512], _f)
+SEMAPHORES = (["sV", "sS", "sT", "sG", "ls"] + ["a%d" % r for r in range(NR)] + ["b%d" % r for r in range(NR)]
+              + ["l%d" % k for k in range(9)] + ["o%d" % k for k in range(5)])
+
+
+def ways(core, T, topo):
+    hop, used = {}, []
+    for d in T.cores:
+        if d == core:
+            continue
+        if topo.may_write(core, d):
+            hop[d] = d
+        else:
+            c = [x for x in topo.cores_of(core) if x != core and x not in used and topo.die(x) == topo.die(core) and topo.may_write(x, d)]
+            hop[d] = c[0]
+            used.append(c[0])
+    return hop
+
+
+def bits(es):
+    m = 0
+    for e in es:
+        m |= 1 << e
+    return m
+
+
+def hop_engines(core, hop, topo):
+    res, out = {}, []
+    for d in hop:
+        if hop[d] == d:
+            res[d] = topo.engines(core, d)
+            out = out + res[d]
+    far = [d for d in hop if hop[d] != d]
+    for k, d in enumerate(far):
+        rest = [e for e in topo.engines(core, hop[d]) if e not in out]
+        n = len(rest) // len(far)
+        res[d] = rest[k * n:(k + 1) * n]
+    return res
+
+
+def relay(g, core, T, topo):
+    local = 0
+    for q, rk in enumerate(T.cores):
+        hop = ways(rk, T, topo)
+        eng = hop_engines(rk, hop, topo)
+        for d in hop:
+            if hop[d] != core or d == core:
+                continue
+            rid, pid = topo.addr(d, core)
+            m = topo.mask(core, d)
+            for r in range(NR):
+                for s, buf, x, w in (("b", T.MB, r * 16 + q * 4, 2), ("a", T.A, (r + 1) * SL + q * 144, 144)):
+                    sem = T.sem["%s%d" % (s, r)]
+                    g.wait_ge(sem, len(eng[d]))
+                    g.remote_dma(buf[:, x:x + w], buf[:, x:x + w], sem, T.sem.ls, pid, rid, m)
+                    local += len(topo.engines(core, d))
+    if local:
+        g.wait_ge(T.sem.ls, local)
+
+
+def rank_program(g, core, T, topo):
+    me = T.rank_of(core)
+    if me is None:
+        relay(g, core, T, topo)
+        return
+    hop = ways(core, T, topo)
+    eng = hop_engines(core, hop, topo)
+    queue = {"V": g.vector, "S": g.scalar, "T": g.tensor, "G": g, "Y": g.sync}
+    count = {"V": 0, "S": 0, "T": 0, "G": 0, "ls": 0}
+    known = {q: {} for q in queue}
+    logs = {}
+
+    def V(name, a=None, b=None, s=1, P=128):
+        t = T[name]
+        if a is None:
+            a, b = 0, t.shape[-1]
+        ap = t[0:P, a:b:s] if s != 1 else t[0:P, a:b]
+        return {"ap": ap, "r": [(name, 0, 512) if name in PSUM else (name, a, b)]}
+
+    def IND(w, o):
+        return {"ap": w["ap"].indirect(o["ap"]), "r": w["r"] + o["r"]}
+
+    def begin(e, outs, ins):
+        recs = {}
+        for views, wr in ((ins, False), (outs, True)):
+            for v in views:
+                for n, a, b in v["r"]:
+                    for (x, y, w, e2, sem, val, clk) in logs.get(n, []):
+                        if x < b and a < y and (wr or w):
+                            if sem not in recs or recs[sem][1] < val:
+                                recs[sem] = (sem, val, clk)
+        k = known[e]
+        for sem, val, clk in sorted(recs.values(), key=lambda z: -len(z[2])):
+            if k.get(sem, 0) < val:
+                queue[e].wait_ge(T.sem[sem], val)
+                k[sem] = val
+                for x in clk:
+                    if k.get(x, 0) < clk[x]:
+                        k[x] = clk[x]
+
+    def done(e, clk, sem, val, outs, ins):
+        clk = dict(clk)
+        clk[sem] = val
+        for views, wr in ((ins, False), (outs, True)):
+            for v in views:
+                for n, a, b in v["r"]:
+                    old = logs.get(n, [])
+                    if wr:
+                        old = [z for z in old if not (a <= z[0] and z[1] <= b)]
+                    else:
+                        old = [z for z in old if z[2] or z[3] != e or not (a <= z[0] and z[1] <= b)]
+                    logs[n] = old + [(a, b, wr, e, sem, val, clk)]
+
+    def op(e, outs, ins, call):
+        begin(e, outs, ins)
+        count[e] += 1
+        call(queue[e]).then_inc(T.sem["s" + e], 1)
+        done(e, known[e], "s" + e, count[e], outs, ins)
+
+    def dma(e, out, in_, sem):
+        begin(e, [out], [in_])
+        queue[e].dma_start(out["ap"], in_["ap"]).then_inc(T.sem[sem], 16)
+        done("dma" + sem, {}, sem, 16, [out], [in_])
+
+    def EXT(ap):
+        return {"ap": ap, "r": []}
+
+    def val(s):
+        return s["ap"] if isinstance(s, dict) else s
+
+    def vs(*a):
+        return [x for x in a if isinstance(x, dict)]
+
+    def ts(out, a, s1, op0, s2=None, op1=None):
+        if op1 is None:
+            op("V", [out], vs(a, s1), lambda q: q.tensor_scalar(out["ap"], a["ap"], val(s1), None, op0))
+        else:
+            op("V", [out], vs(a, s1, s2), lambda q: q.tensor_scalar(out["ap"], a["ap"], val(s1), val(s2), op0, op1))
+
+    def tt(out, a, b, o):
+        op("V", [out], [a, b], lambda q: q.tensor_tensor(out["ap"], a["ap"], b["ap"], o))
+
+    def cp(out, a):
+        op("V", [out], [a], lambda q: q.tensor_copy(out["ap"], a["ap"]))
+
+    def red(out, a, o):
+        op("V", [out], [a], lambda q: q.tensor_reduce(out["ap"], a["ap"], AxisListType.X, o))
+
+    def fill(out, c):
+        op("V", [out], [], lambda q: q.memset(out["ap"], c))
+
+    def scan(out, a, z, op0, op1):
+        op("V", [out], [a, z], lambda q: q.tensor_tensor_scan(out["ap"], a["ap"], z["ap"], 0.0, op0, op1))
+
+    def act(out, a, f, bias=None, scale=None, acc=None):
+        kw = {}
+        if bias is not None:
+            kw["bias"] = val(bias)
+        if scale is not None:
+            kw["scale"] = scale
+        if acc is not None:
+            kw["accum_out"] = acc["ap"]
+        op("S", vs(out, acc), vs(a, bias), lambda q: q.activation(out["ap"], a["ap"], f, **kw))
+
+    def mm(out, pairs, start=True, stop=True):
+        n = len(pairs)
+
+        def call(q):
+            x = None
+            for k, (l, r) in enumerate(pairs):
+                x = q.matmul(out["ap"], l["ap"], r["ap"], start and k == 0, stop and k == n - 1)
+            return x
+        op("T", [out], [v for p in pairs for v in p], call)
+
+    def iota(out, pattern, base, cm):
+        op("G", [out], [], lambda q: q.iota(out["ap"], pattern, base, cm, allow_small_or_imprecise_dtypes=True))
+
+    def sel(out, a, pattern, cmp_, base, cm):
+        op("G", [out], [a], lambda q: q.affine_select(out["ap"], a["ap"], pattern, cmp_, 0.0, base, cm))
+
+    def wrap(base, buf, i, w=512, x=0):
+        return (V(base, 15 - i, 143 - i), V(buf, x + i, x + w, 16))
+
+    def wraps(base, buf, w=512, x=0):
+        return [wrap(base, buf, i, w, x) for i in range(16)]
+
+    def send(r, s, src, dst, w):
+        begin("G", [], [V(src, a, b) for a, b in w.values()])
+        tr = []
+        for d in hop:
+            rid, pid = topo.addr(hop[d], core)
+            a, b = w[d]
+            tr.append(RemoteDMATransfer(dst_ids=[DstId(rid=rid, pnc=pid)], dma_engine_mask=bits(eng[d]), remote_sem=T.sem["%s%d" % (s, r)],
+                                        src=T[src][:, a:b], dst=T[dst[0]][:, dst[1]:dst[2]]))
+            count["ls"] += len(eng[d])
+        g.remote_dma_fused(tr, local_sem=T.sem.ls)
+
+    def arrive(r, s, name, spans):
+        n = 0
+        for c in T.cores:
+            if c != core:
+                h = ways(c, T, topo)
+                n += len(hop_engines(c, h, topo)[core]) if h[core] == core else len(topo.engines(h[core], core))
+        sem = "%s%d" % (s, r)
+        for a, b in spans:
+            logs[name] = logs.get(name, []) + [(a, b, True, "net", sem, n, {sem: n})]
+
+    dma("Y", V("F8I", P=8), EXT(T.f0[:, :]), "l0")
+    for q in range(4):
+        dma("Y", V("A", q * 144, q * 144 + 128), EXT(T.s0[:, q * 128:q * 128 + 128]), "l%d" % (1 + q))
+    for q in range(4):
+        dma("S" if q % 2 else "Y", V("OPW", q * 1024, q * 1024 + 1024), EXT(T.opr[:, q * 1024:q * 1024 + 1024]), "l%d" % (5 + q))
+
+    fill(V("ONE"), 1.0)
+    iota(V("LI", 0, 1), [[1, 1]], 0, 1)
+    iota(V("LM"), [[1, 16]], 0, 0)
+    iota(V("CL", 0, 32), [[144, 4], [16, 8]], 0, 0)
+    iota(V("CL", 32, 40), [[8, 2], [0, 2], [288, 2]], 128, 0)
+    sel(V("S1"), V("ONE", 0, 144), [[0, 9], [1, 16]], O.is_equal, -15, 0)
+    sel(V("S1"), V("S1"), [[-16, 9], [0, 16]], O.is_ge, 0, 1)
+    sel(V("S1"), V("S1"), [[16, 9], [0, 16]], O.is_ge, 15, -1)
+    sel(V("B8", P=8), V("ONE", 0, 144, P=8), [[0, 9], [1, 16]], O.is_equal, -15, 0)
+    sel(V("B8", P=8), V("B8", P=8), [[1, 9], [0, 16]], O.is_equal, 0, -1)
+    sel(V("ID"), V("ONE", 0, 128), [[-1, 128]], O.is_equal, 0, 1)
+    sel(V("BLK"), V("ONE", 0, 128), [[-16, 8], [0, 16]], O.is_ge, 0, 1)
+    sel(V("BLK"), V("BLK"), [[16, 8], [0, 16]], O.is_ge, 15, -1)
+    sel(V("NUT"), V("BLK"), [[-1, 128]], O.is_gt, 0, 1)
+    iota(V("DM"), [[0, 4], [1, 16]], 0, 0)
+    iota(V("K"), [[0, 4], [1, 128]], 0, 0)
+    iota(V("O32"), [[32, 4], [0, 8]], 0, 0)
+    iota(V("O272"), [[272, 4], [0, 8]], 0, 0)
+    iota(V("K1"), [[0, 4], [1, 128]], 1, 0)
+    iota(V("B8C"), [[8, 12], [0, 8]], 0, 0)
+    iota(V("B256"), [[256, 12], [0, 8]], 128, 0)
+    iota(V("DM3"), [[0, 12], [1, 8]], 0, 0)
+    sel(V("G8"), V("ONE", 0, 8), [[-16, 8]], O.is_ge, 0, 1)
+    sel(V("G8"), V("G8"), [[16, 8]], O.is_ge, 15, -1)
+    for i in range(16):
+        fill(V("WR", i, i + 1), float(WT[i]))
+    for o in range(3):
+        fill(V("E8C", o, o + 1), 811.0 * o)
+    ts(V("LI", 1, 2), V("LI", 0, 1), 15, O.bitwise_and)
+    lane = V("LC", 0, 1)
+    cp(lane, V("LI", 1, 2))
+    ts(V("LI", 2, 3), V("LI", 1, 2), 7, O.bitwise_and)
+    ts(V("LI", 3, 4), V("LI", 1, 2), 3, O.arith_shift_right)
+    ts(V("LM"), V("LM"), lane, O.is_equal)
+    ts(V("LC", 3, 4), V("LI", 3, 4), 144.0, O.mult)
+    tt(V("W2"), V("WR"), V("LM"), O.mult)
+    tt(V("LC", 4, 5), V("LC", 3, 4), V("LI", 2, 3), O.add)
+    red(V("LC", 1, 2), V("W2"), O.add)
+    ts(V("CL", 0, 32), V("CL", 0, 32), lane, O.add)
+    ts(V("CL", 32, 40), V("CL", 32, 40), V("LC", 4, 5), O.add)
+    cp(V("LI", 4, 5), V("LC", 1, 2))
+    ts(V("LI", 5, 6), V("LI", 4, 5), 3, O.bitwise_and)
+    ts(V("LC", 2, 3), V("LI", 5, 6), -1.0, O.mult, 1026.0, O.add)
+    ts(V("WM"), V("S1"), V("LC", 1, 2), O.mult)
+    ts(V("F8", P=8), V("F8I", P=8), -1023.0, O.add)
+    ts(V("B8", P=8), V("B8", P=8), 1.0 / 32, O.mult)
+
+    def consts1():
+        ts(V("XB"), V("S1"), V("LC", 2, 3), O.mult)
+        ts(V("IDF"), V("ID"), 131072.0, O.mult)
+        ts(V("IDN"), V("ID"), -1.0, O.mult)
+        for o in range(4):
+            fill(V("BO", o, o + 1), -8192.0 * o)
+        fill(V("CH", 4096, 4112), 0.0)
+
+    def consts2():
+        cp(V("BLKF"), V("BLK"))
+        ts(V("NUT"), V("NUT"), -1.0, O.mult)
+        ts(V("ID16"), V("ID"), 16.0, O.mult)
+        ts(V("SD"), V("S1"), lane, O.mult)
+        ts(V("S32"), V("S1"), 1.0 / 32, O.mult)
+        ts(V("DM"), V("DM"), lane, O.is_equal)
+        fill(V("ZERO"), 0.0)
+        fill(V("YW", 256, 272), 0.0)
+        fill(V("W"), 0.0)
+        fill(V("EBW"), 1000.0)
+
+    def consts3():
+        fill(V("A", EMPTY * SL, EMPTY * SL + SL), 0.0)
+        ts(V("LC", 6, 7), lane, -128.0, O.add)
+        ts(V("RM"), V("DM3"), 0.0, O.is_gt)
+        ts(V("DM3"), V("DM3"), lane, O.is_equal)
+        ts(V("LC", 5, 6), lane, 6.5, O.is_gt, 1000.0, O.mult)
+        ts(V("SE"), V("S1"), V("LC", 6, 7), O.mult)
+        ts(V("G8F"), V("G8"), 1.0 / 16, O.mult)
+        ts(V("G8"), V("G8"), 32.0, O.mult)
+        fill(V("S3"), 0.0)
+
+    def C(k):
+        return V("SV", k, k + 1)
+
+    def w_(k, n=1):
+        return V("SW", k, k + n)
+
+    LO, HI, PT, U, EE, EL, ER = V("SV", 0, 3), V("SV", 4, 7), V("SV", 8, 11), C(12), V("SV", 17, 20), V("SV", 18, 21), V("SV", 16, 19)
+    LOE, BASE, E8, CC, LIM, LMN, THR = C(24), C(25), C(26), C(27), C(28), C(29), C(30)
+    fill(V("SV"), 0.0)
+    fill(U, 1023.0)
+    fill(C(3), 100000.0)
+    fill(C(17), 1.0)
+    fill(V("SV", 9, 12), float(EMPTY * SL))
+
+    def dot(out, a, k):
+        tt(w_(k, 3), a, EE, O.mult)
+        red(out, w_(k, 3), O.add)
+
+    def split(o, buf, x):
+        p = V("PN", o * 8, o * 8 + 8)
+        ts(V(buf, x, x + 8), p, MAGIC, O.add, MAGIC, O.subtract)
+        tt(V(buf, x + 8, x + 16), p, V(buf, x, x + 8), O.subtract)
+
+    mm(V("PN", 0, 32), [(V("B8", 15 - i, 143 - i, P=8), V("F8", i, 512, 16, P=8)) for i in range(16)])
+    for q in range(4):
+        split(q, "A", q * 144 + 128)
+    dot(BASE, PT, 0)
+
+    def parents(r):
+        if r:
+            level_a(r - 1)
+            dot(BASE, PT, 0)
+        ts(V("OFA"), V("CL"), BASE, O.add)
+        lay = V("A", 0, (r + 1) * SL)
+        cp(V("S", 0, 256), IND(lay, V("OFA", 0, 16)))
+        act(V("S", 256, 512), IND(lay, V("OFA", 16, 32)), F.Copy)
+        act(V("FS"), IND(lay, V("OFA", 32, 40)), F.Copy)
+        mm(V("PU", 0, 32), wraps("WM", "S"))
+        dot(E8, V("E8C", 0, 3), 3)
+        dot(THR, V("SV", 3, 6), 9)
+        ts(THR, THR, -1023.0, O.add, 1.0 / 32, O.mult)
+        tt(V("T8"), V("FS", 0, 64), V("FS", 64, 128), O.add)
+        ts(V("P8"), V("T8"), THR, O.is_ge, 32.0, O.mult)
+        tt(V("FS", 0, 64), V("FS", 0, 64), V("P8"), O.add)
+        if not r:
+            consts1()
+        for k in range(2):
+            mm(V("PC%d" % k, 0, 512), [(V("IDN"), V("S"))], True, False)
+
+    def pre(r):
+        tt(w_(22, 3), V("SV", 9, 12), EE, O.mult)
+        ts(w_(19, 3), EE, float((r + 1) * SL), O.mult)
+        ts(w_(13, 3), EE, -1.0, O.mult, 1.0, O.add)
+        ts(w_(36), LOE, 1.0, O.add)
+        ts(w_(38), C(17), -1.0, O.mult, 1.0, O.add)
+        ts(w_(40, 3), LO, 1.0, O.add)
+        tt(w_(19, 3), w_(19, 3), w_(22, 3), O.subtract)
+        tt(HI, HI, w_(13, 3), O.mult)
+        tt(V("SV", 9, 12), V("SV", 9, 12), w_(19, 3), O.add)
+
+    def level_a(r):
+        B, m, rt, lp, bk, up, st = [w_(k) for k in (10, 11, 27, 28, 29, 30, 39)]
+        red(w_(12), V("MB", r * 16 + 1, r * 16 + 16, 4), O.min)
+        red(B, V("MB", r * 16, r * 16 + 16, 4), O.min)
+        ts(V("MD"), V("LM"), w_(12), O.mult)
+        mm(V("PN", 0, 16), [(V("BLKF"), V("MD"))])
+        ts(w_(13, 3), EE, B, O.mult)
+        tt(lp, w_(36), B, O.max)
+        tt(HI, HI, w_(13, 3), O.add)
+        red(m, V("PN", 0, 16), O.min)
+        tt(w_(26), m, B, O.is_lt)
+        tt(w_(35), m, B, O.is_ge)
+        tt(w_(31), w_(26), C(19), O.mult)
+        tt(w_(35), w_(35), C(19), O.max)
+        ts(w_(32), w_(31), -4000.0, O.mult, 4000.0, O.add)
+        tt(w_(33), w_(32), m, O.max)
+        tt(U, U, w_(33), O.min)
+        tt(w_(34), m, U, O.is_ge)
+        tt(w_(37), lp, U, O.is_ge)
+        tt(rt, w_(34), w_(35), O.max)
+        tt(w_(37), w_(37), w_(38), O.mult)
+        ts(up, rt, -1.0, O.mult, 1.0, O.add)
+        tt(bk, w_(37), rt, O.mult)
+        ts(w_(46, 3), ER, up, O.mult)
+        tt(st, rt, bk, O.subtract)
+        ts(w_(49, 3), EL, bk, O.mult)
+        ts(w_(43, 3), EE, bk, O.mult)
+        ts(w_(52, 3), EE, st, O.mult)
+        ts(w_(55, 3), EE, st, O.mult, lp, O.mult)
+        tt(w_(16, 3), w_(46, 3), w_(49, 3), O.add)
+        tt(EE, w_(16, 3), w_(52, 3), O.add)
+
+    def level_b():
+        tt(w_(40, 3), w_(40, 3), HI, O.max)
+        tt(w_(43, 3), w_(43, 3), EE, O.add)
+        ts(w_(43, 3), w_(43, 3), -1.0, O.mult, 1.0, O.add)
+        tt(w_(40, 3), w_(40, 3), w_(49, 3), O.mult)
+        tt(LO, LO, w_(43, 3), O.mult)
+        tt(w_(40, 3), w_(40, 3), w_(55, 3), O.add)
+        tt(LO, LO, w_(40, 3), O.add)
+
+    def rnd(r):
+        parents(r)
+        cp(V("UI"), V("PU", 0, 32))
+        ts(V("UU"), V("UI"), 4095, O.bitwise_and)
+        cp(V("UF"), V("UU"))
+        tt(V("USQ"), V("UU"), V("UU"), O.mult)
+        ts(V("BB"), V("USQ"), 4, O.arith_shift_right)
+        for j in range(8):
+            act(V("TJ", j * 32, j * 32 + 32), V("UF"), F.Identity, bias=E8, scale=float(KA[j]))
+
+        def numbers(j0, j1):
+            for j in range(j0, j1):
+                tt(V("VJ", j * 32, j * 32 + 32), V("TJ", j * 32, j * 32 + 32), V("BB"), O.add)
+            a, b = j0 * 32, j1 * 32
+            ts(V("VK", a, b), V("VJ", a, b), 4095, O.bitwise_and)
+            cp(V("OFO", a, b), V("VK", a, b))
+
+        def gather(k):
+            x, y = k * 512, k * 512 + 512
+            tt(V("D", x, y), IND(V("OPW"), V("OFO", k * 32, k * 32 + 32)), V("S"), O.subtract)
+
+        def other(k):
+            z = k // 2 * 512
+            act(V("GA", z, z + 512), IND(V("OPW"), V("OFO", k * 32, k * 32 + 32)), F.Copy)
+            mm(V("PC%d" % (k // 2), 0, 512), [(V("ID"), V("GA", z, z + 512))], False, True)
+
+        def size(k):
+            x, y = k * 512, k * 512 + 512
+            act(V("CH", x, y), V("PC%d" % (k // 2), 0, 512) if k in (1, 3) else V("D", x, y), F.Abs)
+
+        def sums(k):
+            mm(V("PX" if k < 2 else "PEA", k * 64, k * 64 + 64), [(V("IDF"), V("FS", 0, 64)), (V("IDF"), V("FS", 64, 128))]
+               + wraps("XB", "CH", 1024, k * 1024))
+
+        numbers(0, 2)
+        other(1)
+        gather(0)
+        size(0)
+        size(1)
+        sums(0)
+        numbers(2, 8)
+        other(3)
+        for k in (2, 4, 5, 6, 7):
+            gather(k)
+        size(2)
+        size(3)
+        sums(1)
+        for k in (4, 5, 6, 7):
+            size(k)
+            if k % 2:
+                sums(k // 2)
+        if r:
+            level_b()
+        dot(LOE, LO, 6)
+        ts(CC, LOE, -4096.0, O.mult, 444.0 + 4096.0 * 1023, O.add)
+        ts(LIM, LOE, -1.0, O.mult, 1022.5, O.add)
+        ts(LMN, LOE, -1023.0, O.add)
+        if not r:
+            consts2()
+        fill(V("TT"), 511.5)
+        for p, a, b in (("PX", 0, 128), ("PEA", 128, 256)):
+            ts(V("XI", a, b), V(p, a, b), CC, O.add)
+            ts(V("OW", a, b), V("XI", a, b), 3, O.bitwise_and)
+            ts(V("Y", a, b), V("XI", a, b), 12, O.arith_shift_right, 4095, O.bitwise_and)
+            ts(V("OW4", a, b), V("OW", a, b), 8192.0, O.mult)
+            tt(V("Z", a, b), V("Y", a, b), V("OW4", a, b), O.add)
+        for o in (2, 0, 1):
+            act(V("X", o * 256, o * 256 + 256), V("Z"), F.Abs, bias=V("BO", o, o + 1))
+        ts(V("OW3"), V("OW"), 3.0, O.not_equal, 8192.0, O.mult)
+        tt(V("XH", 256, 512), V("OW3"), V("Y"), O.add)
+        cp(V("XH", 0, 256), V("X", 512, 768))
+        s = 512
+        while s:
+            for o in (0, 1):
+                act(V("DA", o * 256, o * 256 + 256), V("X", o * 256, o * 256 + 256), F.Sign, bias=V("TT", o, o + 1), scale=-1.0, acc=V("CN", o, o + 1))
+            for o in (3, 2):
+                z = o * 256 - 512
+                ts(V("DV", z, z + 256), V("XH", z, z + 256), V("TT", o, o + 1), O.is_lt)
+                mm(V("PC%d" % (o - 2), 0, 64), [(V("BLK"), V("DV", z + 64 * x, z + 64 * x + 64)) for x in range(4)])
+            mm(V("PN", 0, 2), [(V("BLKF"), V("CN", 0, 2))])
+            ts(V("TTH"), V("TT"), -s / 2.0 if s > 1 else -1.0, O.add)
+            for o in (3, 2):
+                red(V("CN", o, o + 1), V("PC%d" % (o - 2), 0, 64), O.add)
+            ts(V("TU", 2, 4), V("CN", 2, 4), 128.5, O.is_le, float(s), O.mult)
+            tt(V("TT", 2, 4), V("TTH", 2, 4), V("TU", 2, 4), O.add)
+            ts(V("TU", 0, 2), V("PN", 0, 2), -3839.5, O.is_le, float(s), O.mult)
+            tt(V("TT", 0, 2), V("TTH", 0, 2), V("TU", 0, 2), O.add)
+            s //= 2
+        ts(V("TTH"), V("TT"), LIM, O.min)
+        for o in (2, 3, 0, 1):
+            ts(V("KP", o * 256, o * 256 + 256), V("X", o * 256, o * 256 + 256) if o < 2 else V("XH", o * 256 - 512, o * 256 - 256), V("TTH", o, o + 1), O.is_lt)
+        for o in (2, 3, 0, 1):
+            scan(V("R", o * 256, o * 256 + 256), V("KP", o * 256, o * 256 + 256), V("ZERO"), O.add, O.add)
+
+        def places(o):
+            mm(V("PC%d" % (o // 2), o % 2 * 256, o % 2 * 256 + 256), [(V("BLK"), V("R", o * 256, o * 256 + 256)), (V("NUT"), V("KP", o * 256, o * 256 + 256))])
+
+        def heads(o):
+            tt(V("W", o * 272, o * 272 + 256), V("PC%d" % (o // 2), o % 2 * 256, o % 2 * 256 + 256), V("KP", o * 256, o * 256 + 256), O.mult)
+
+        places(2)
+        mm(V("PEA", 0, 64), [(V("BLK"), V("R", 15, 1024, 16))])
+        mm(V("PEB", 0, 64), [wrap("S1", "R", b, 1024) for b in range(16)])
+        tt(V("EM", 0, 64), V("PEA", 0, 64), V("DM"), O.mult)
+        for o in range(4):
+            red(V("EA", o, o + 1), V("EM", o * 16, o * 16 + 16), O.add)
+        for o in range(4):
+            ts(V("IA", o * 128, o * 128 + 128), V("K", 0, 128), V("EA", o, o + 1), O.is_ge)
+        mm(V("PL", 0, 32), [(V("ID"), V("O32"))] + wraps("S1", "IA"))
+        for o in range(4):
+            act(V("EBW", o * 32, o * 32 + 16), V("PEB", o * 16, o * 16 + 16), F.Copy)
+        mb = r * 16 + me * 4
+        red(w_(61), V("TTH"), O.min)
+        red(w_(60), V("Y"), O.min)
+        ts(V("MB", mb, mb + 1), w_(61), LOE, O.add, 0.5, O.add)
+        ts(V("MB", mb + 1, mb + 2), w_(60), LOE, O.add, 1023.0, O.min)
+        send(r, "b", "MB", ("MB", mb, mb + 2), {d: (mb, mb + 2) for d in hop})
+        arrive(r, "b", "MB", [(r * 16 + q * 4, r * 16 + q * 4 + 2) for q in range(4) if q != me])
+        ts(V("YW", 0, 256), V("Y"), LMN, O.add)
+        cp(V("OFB"), V("PL", 0, 32))
+        tt(V("AB", 0, 32), V("PL", 0, 32), V("O32"), O.subtract)
+        places(3)
+        tt(V("IB"), IND(V("EBW"), V("OFB")), V("K"), O.is_le)
+        mm(V("PL", 0, 32), [(V("ID"), V("O272")), (V("ID16"), V("AB", 0, 32))] + wraps("S1", "IB"))
+        places(0)
+        places(1)
+        heads(2)
+        heads(3)
+        ts(V("OFV"), V("PL", 16, 32), -544.0, O.add)
+        cp(V("OFW", 0, 16), V("PL", 0, 16))
+        tt(V("CB"), V("PL", 0, 32), V("O272"), O.subtract)
+        cp(V("OFC"), V("CB"))
+        tt(V("OH", 256, 512), IND(V("W", 544, 1088), V("OFV")), V("K1", 0, 256), O.is_equal)
+        heads(0)
+        heads(1)
+        tt(V("OH", 0, 256), IND(V("W", 0, 544), V("OFW", 0, 16)), V("K1", 0, 256), O.is_equal)
+        mm(V("PU", 0, 32), [(V("ID16"), V("CB"))] + wraps("SD", "OH"))
+        tt(V("CG", 0, 512), IND(V("YW"), V("OFC")), V("OH", 0, 512), O.mult)
+        mm(V("PN", 0, 32), wraps("S32", "CG"))
+        cp(V("OFN"), V("PU", 0, 32))
+        blk = {}
+        for o in range(4):
+            blk[T.cores[o]] = ("A", (r + 1) * SL + me * 144) if o == me else ("SND", r * SL + o * 144)
+        far = [d for d in hop] + [core]
+        for k, d in enumerate(far):
+            n, x = blk[d]
+            o = T.cores.index(d)
+            v = IND(V("CH"), V("OFN", o * 8, o * 8 + 8))
+            if k == 1:
+                cp(V(n, x, x + 128), v)
+            else:
+                act(V(n, x, x + 128), v, F.Copy)
+        pre(r)
+        for d in far:
+            n, x = blk[d]
+            split(T.cores.index(d), n, x + 128)
+            if d == far[2]:
+                x = (r + 1) * SL + me * 144
+                send(r, "a", "SND", ("A", x, x + 144), {d: (blk[d][1], blk[d][1] + 144) for d in hop})
+        arrive(r, "a", "A", [((r + 1) * SL + q * 144, (r + 1) * SL + q * 144 + 144) for q in range(4) if q != me])
+        if not r:
+            consts3()
+
+    for r in range(NR):
+        rnd(r)
+    level_a(NR - 1)
+
+    for l in range(3):
+        ts(V("OG3", l * 40, l * 40 + 40), V("CL"), C(9 + l), O.add)
+    ts(w_(0, 3), HI, -1023.0, O.add, 1.0 / 32, O.mult)
+    for l in range(3):
+        cp(V("FF", l * 128, l * 128 + 128), IND(V("A"), V("OG3", l * 40 + 32, l * 40 + 40)))
+    for k in range(12):
+        l, q = k // 4, k % 4
+        act(V("S3", k * 256, k * 256 + 128), IND(V("A"), V("OG3", l * 40 + q * 8, l * 40 + q * 8 + 8)), F.Copy)
+    for l in range(3):
+        a, b = l * 32, l * 32 + 32
+        tt(V("F3", a, b), V("FF", l * 128, l * 128 + 32), V("FF", l * 128 + 64, l * 128 + 96), O.add)
+    for l in range(3):
+        a, b = l * 32, l * 32 + 32
+        ts(V("KP3", a, b), V("F3", a, b), w_(l), O.is_lt)
+    scan(V("R3"), V("RM"), V("KP3"), O.mult, O.add)
+    mm(V("PEA", 0, 96), [(V("BLK"), V("R3"))])
+    mm(V("PC0", 0, 96), [(V("BLK"), V("R3")), (V("NUT"), V("KP3"))])
+    tt(V("EM"), V("PEA", 0, 96), V("DM3"), O.mult)
+    for k in range(12):
+        red(V("EA", k, k + 1), V("EM", k * 8, k * 8 + 8), O.add)
+    ts(V("EA"), V("EA"), V("LC", 5, 6), O.add)
+    for k in range(12):
+        ts(V("IA", k * 128, k * 128 + 128), V("K", 0, 128), V("EA", k, k + 1), O.is_ge)
+    mm(V("PL", 0, 96), [(V("ID"), V("B8C"))] + wraps("S1", "IA", 1536))
+    tt(V("W3"), V("PC0", 0, 96), V("KP3"), O.mult)
+    level_b()
+    cp(V("YT", 0, 3), LO)
+    cp(V("YT", 3, 6), HI)
+    tt(w_(60), C(19), C(19), O.add)
+    tt(V("YT", 6, 7), w_(60), C(18), O.add)
+    cp(V("YT", 7, 8), U)
+    mm(V("PX", 0, 8, P=8), [(V("G8F"), V("YT"))])
+    cp(V("OF3"), V("PL", 0, 96))
+    tt(V("AB"), V("PL", 0, 96), V("B8C"), O.subtract)
+    for l in range(3):
+        a, b = l * 512, l * 512 + 512
+        tt(V("OH", a, b), IND(V("W3"), V("OF3", l * 32, l * 32 + 32)), V("K1"), O.is_equal)
+    mm(V("PU", 0, 96), [(V("ID16"), V("AB")), (V("ID"), V("B256"))] + wraps("SE", "OH", 1536))
+    cp(V("YT8", P=8), V("PX", 0, 8, P=8))
+    dma("Y", EXT(T.yt[:, :]), V("YT8", P=8), "o0")
+
+    def costs(l):
+        a, b = l * 512, l * 512 + 512
+        tt(V("CG", a, b), IND(V("F3"), V("OF3", l * 32, l * 32 + 32)), V("OH", a, b), O.mult)
+        p = ("PC0", "PC1", "PEB")[l]
+        mm(V(p, 0, 512, P=8), [(V("G8"), V("CG", a, b))])
+
+    costs(0)
+    cp(V("OP3"), V("PU", 0, 96))
+    for l in range(3):
+        a, b = l * 512, l * 512 + 512
+        act(V("YL", a, b), IND(V("S3"), V("OP3", l * 32, l * 32 + 32)), F.Copy)
+        dma("Y", EXT(T.yl[:, a:b]), V("YL", a, b), "o%d" % (1 + l))
+    costs(1)
+    costs(2)
+    for l in range(3):
+        a, b = l * 512, l * 512 + 512
+        ts(V("YF", a, b, P=8), V(("PC0", "PC1", "PEB")[l], 0, 512, P=8), 1023.0, O.add)
+    dma("S", EXT(T.yf[:, :]), V("YF", P=8), "o4")
+    for k in range(4):
+        g.sync.wait_ge(T.sem["o%d" % k], 16)
+    for k in range(9):
+        g.sync.wait_ge(T.sem["l%d" % k], 16)
+    g.scalar.wait_ge(T.sem.o4, 16)
+    for e in ("V", "S", "T", "G"):
+        g.wait_ge(T.sem["s" + e], count[e])
+    g.wait_ge(T.sem.ls, count["ls"])

@@ -16,14 +16,15 @@ for _n, _w, _d in (
         ("GA", 1024, _b), ("CH", 4112, _b), ("OFA", 40, _u), ("OFO", 256, _u), ("OFB", 32, _u), ("OFW", 32, _u), ("OFV", 16, _u),
         ("OFC", 32, _u), ("OFN", 32, _u), ("UI", 32, _i), ("UU", 32, _i), ("UF", 32, _f), ("USQ", 32, _i), ("BB", 32, _i),
         ("TJ", 256, _f), ("VJ", 256, _i), ("VK", 256, _i), ("XI", 256, _i), ("Y", 256, _i), ("OW", 256, _i), ("OW3", 256, _f), ("OW4", 256, _f),
-        ("Z", 256, _f), ("YW", 272, _f), ("X", 768, _f), ("XH", 512, _h), ("DA", 512, _b), ("DV", 512, _b), ("KP", 1024, _b), ("R", 1024, _b),
+        ("Z", 256, _f), ("YW", 272, _f), ("X", 768, _f), ("XH", 1024, _h), ("DA", 512, _b), ("DV", 512, _b), ("KP", 1024, _b), ("R", 1024, _b),
         ("W", 1088, _b), ("IA", 1536, _b), ("IB", 512, _b), ("OH", 1536, _b), ("CG", 1536, _h), ("EBW", 128, _b), ("AB", 96, _b), ("CB", 32, _b),
-        ("EM", 96, _f), ("EA", 12, _f), ("T8", 64, _f), ("P8", 64, _f), ("TT", 4, _f), ("TTH", 4, _f), ("TU", 4, _f), ("CN", 4, _f),
+        ("EM", 96, _f), ("EA", 12, _f), ("T8", 64, _f), ("P8", 64, _f), ("TT", 4, _f), ("TLO", 4, _f), ("THI", 4, _f), ("CN", 4, _f), ("QN", 4, _f),
         ("SV", 64, _f), ("SW", 64, _f), ("MD", 16, _f),
-        ("ONE", 256, _b), ("ZERO", 256, _b), ("BLK", 128, _b), ("BLKF", 128, _f), ("NUT", 128, _b), ("ID", 128, _b), ("IDN", 128, _b),
-        ("IDF", 128, _b), ("ID16", 128, _b), ("S1", 144, _b), ("SD", 144, _b), ("SE", 144, _b), ("S32", 144, _h), ("WM", 144, _b), ("XB", 144, _h),
-        ("K", 512, _b), ("K1", 512, _b), ("CL", 40, _f), ("O32", 32, _b), ("O272", 32, _b), ("DM", 64, _f), ("LM", 16, _f), ("WR", 16, _f),
-        ("W2", 16, _f), ("LC", 16, _f), ("LI", 8, _i), ("BO", 4, _f), ("E8C", 4, _f), ("G8", 8, _h), ("G8F", 8, _f),
+        ("ONE", 256, _b), ("ZERO", 256, _b), ("BLK", 128, _b), ("BLKF", 128, _f), ("NBF", 128, _f), ("NB", 128, _b), ("CQ", 2, _b), ("CA", 2, _b),
+        ("NUT", 128, _b), ("ID", 128, _b), ("IDN", 128, _b), ("IDF", 128, _b), ("ID16", 128, _b), ("S1", 144, _b), ("SD", 144, _b), ("SE", 144, _b),
+        ("S32", 144, _h), ("WM", 144, _b), ("XB", 144, _h), ("K", 512, _b), ("K1", 512, _b), ("CL", 40, _f), ("O32", 32, _b), ("O272", 32, _b),
+        ("DM", 64, _f), ("LM", 16, _f), ("WR", 16, _f), ("W2", 16, _f), ("LC", 16, _f), ("LI", 8, _i), ("BO", 4, _f), ("E8C", 4, _f),
+        ("G8", 8, _h), ("G8F", 8, _f),
         ("S3", 3072, _b), ("FF", 384, _b), ("F3", 96, _f), ("KP3", 96, _b), ("R3", 96, _b), ("RM", 96, _b), ("W3", 96, _b),
         ("OF3", 96, _u), ("OG3", 120, _u), ("OP3", 96, _u), ("B8C", 96, _b), ("B256", 96, _b), ("DM3", 96, _f), ("YL", 1536, _b), ("YT", 8, _f)):
     SCRATCH[_n] = ("sbuf", [128, _w], _d)
@@ -31,7 +32,7 @@ for _n, _w, _d in (("B8", 144, _h), ("F8I", 512, _i), ("F8", 512, _h), ("YF", 15
     SCRATCH[_n] = ("sbuf", [8, _w], _d)
 for _n in PSUM:
     SCRATCH[_n] = ("psum", [128, 512], _f)
-SEMAPHORES = (["sV", "sS", "sT", "sG", "ls"] + ["a%d" % r for r in range(NR)] + ["b%d" % r for r in range(NR)]
+SEMAPHORES = (["sV", "sS", "sT", "sG", "ls"] + ["%s%d" % (s, r) for s in "ab" for r in range(NR)]
               + ["l%d" % k for k in range(9)] + ["o%d" % k for k in range(5)])
 
 
@@ -56,15 +57,12 @@ def bits(es):
     return m
 
 
-def hop_engines(core, hop, topo):
-    res, out = {}, []
-    for d in hop:
-        if hop[d] == d:
-            res[d] = topo.engines(core, d)
-            out = out + res[d]
+def hop_engines(core, hop, topo, s):
     far = [d for d in hop if hop[d] != d]
+    res = {d: topo.engines(core, d) for d in hop if hop[d] == d}
+    used = [] if s == "a" else [e for d in res for e in res[d]]
     for k, d in enumerate(far):
-        rest = [e for e in topo.engines(core, hop[d]) if e not in out]
+        rest = [e for e in topo.engines(core, hop[d]) if e not in used]
         n = len(rest) // len(far)
         res[d] = rest[k * n:(k + 1) * n]
     return res
@@ -74,7 +72,6 @@ def relay(g, core, T, topo):
     local = 0
     for q, rk in enumerate(T.cores):
         hop = ways(rk, T, topo)
-        eng = hop_engines(rk, hop, topo)
         for d in hop:
             if hop[d] != core or d == core:
                 continue
@@ -83,7 +80,7 @@ def relay(g, core, T, topo):
             for r in range(NR):
                 for s, buf, x, w in (("b", T.MB, r * 16 + q * 4, 2), ("a", T.A, (r + 1) * SL + q * 144, 144)):
                     sem = T.sem["%s%d" % (s, r)]
-                    g.wait_ge(sem, len(eng[d]))
+                    g.wait_ge(sem, len(hop_engines(rk, hop, topo, s)[d]))
                     g.remote_dma(buf[:, x:x + w], buf[:, x:x + w], sem, T.sem.ls, pid, rid, m)
                     local += len(topo.engines(core, d))
     if local:
@@ -96,7 +93,6 @@ def rank_program(g, core, T, topo):
         relay(g, core, T, topo)
         return
     hop = ways(core, T, topo)
-    eng = hop_engines(core, hop, topo)
     queue = {"V": g.vector, "S": g.scalar, "T": g.tensor, "G": g, "Y": g.sync}
     count = {"V": 0, "S": 0, "T": 0, "G": 0, "ls": 0}
     known = {q: {} for q in queue}
@@ -204,6 +200,10 @@ def rank_program(g, core, T, topo):
             return x
         op("T", [out], [v for p in pairs for v in p], call)
 
+    def mm2(out, early, late):
+        mm(out, early, True, False)
+        mm(out, late, False, True)
+
     def iota(out, pattern, base, cm):
         op("G", [out], [], lambda q: q.iota(out["ap"], pattern, base, cm, allow_small_or_imprecise_dtypes=True))
 
@@ -216,30 +216,33 @@ def rank_program(g, core, T, topo):
     def wraps(base, buf, w=512, x=0):
         return [wrap(base, buf, i, w, x) for i in range(16)]
 
-    def send(r, s, src, dst, w):
-        begin("G", [], [V(src, a, b) for a, b in w.values()])
-        tr = []
-        for d in hop:
-            rid, pid = topo.addr(hop[d], core)
-            a, b = w[d]
-            tr.append(RemoteDMATransfer(dst_ids=[DstId(rid=rid, pnc=pid)], dma_engine_mask=bits(eng[d]), remote_sem=T.sem["%s%d" % (s, r)],
-                                        src=T[src][:, a:b], dst=T[dst[0]][:, dst[1]:dst[2]]))
-            count["ls"] += len(eng[d])
-        g.remote_dma_fused(tr, local_sem=T.sem.ls)
+    def send(r, s, src, dst, w, width):
+        begin("G", [], [V(src, w[d], w[d] + width) for d in hop])
+        eng = hop_engines(core, hop, topo, s)
+        far, near = [d for d in hop if hop[d] != d], [d for d in hop if hop[d] == d]
+        for ds in ([far, near] if s == "a" else [far + near]):
+            tr = []
+            for d in ds:
+                rid, pid = topo.addr(hop[d], core)
+                tr.append(RemoteDMATransfer(dst_ids=[DstId(rid=rid, pnc=pid)], dma_engine_mask=bits(eng[d]), remote_sem=T.sem["%s%d" % (s, r)],
+                                            src=T[src][:, w[d]:w[d] + width], dst=T[dst[0]][:, dst[1]:dst[1] + width]))
+                count["ls"] += len(eng[d])
+            g.remote_dma_fused(tr, local_sem=T.sem.ls)
 
-    def arrive(r, s, name, spans):
+    def arrive(r, s, name, x, stride, width):
         n = 0
         for c in T.cores:
             if c != core:
                 h = ways(c, T, topo)
-                n += len(hop_engines(c, h, topo)[core]) if h[core] == core else len(topo.engines(h[core], core))
+                n += len(hop_engines(c, h, topo, s)[core]) if h[core] == core else len(topo.engines(h[core], core))
         sem = "%s%d" % (s, r)
-        for a, b in spans:
-            logs[name] = logs.get(name, []) + [(a, b, True, "net", sem, n, {sem: n})]
+        for q in range(4):
+            if q != me:
+                logs[name] = logs.get(name, []) + [(x + q * stride, x + q * stride + width, True, "net", sem, n, {sem: n})]
 
     dma("Y", V("F8I", P=8), EXT(T.f0[:, :]), "l0")
     for q in range(4):
-        dma("Y", V("A", q * 144, q * 144 + 128), EXT(T.s0[:, q * 128:q * 128 + 128]), "l%d" % (1 + q))
+        dma("Y" if q % 2 else "S", V("A", q * 144, q * 144 + 128), EXT(T.s0[:, q * 128:q * 128 + 128]), "l%d" % (1 + q))
     for q in range(4):
         dma("S" if q % 2 else "Y", V("OPW", q * 1024, q * 1024 + 1024), EXT(T.opr[:, q * 1024:q * 1024 + 1024]), "l%d" % (5 + q))
 
@@ -300,6 +303,14 @@ def rank_program(g, core, T, topo):
 
     def consts2():
         cp(V("BLKF"), V("BLK"))
+        ts(V("NBF"), V("BLK"), -4096.0, O.mult)
+        ts(V("NB"), V("BLK"), -4096.0, O.mult)
+        fill(V("CQ", 0, 1), 524288.0)
+        fill(V("CQ", 1, 2), 2048.0)
+        ts(V("LC", 8, 9), lane, 0.0, O.is_equal, -15728640.0, O.mult)
+        ts(V("LC", 9, 10), lane, 1.0, O.is_equal, 4096.0, O.mult)
+        for o in range(2):
+            tt(V("CA", o, o + 1), V("LC", 8, 9), V("LC", 9, 10), O.add)
         ts(V("NUT"), V("NUT"), -1.0, O.mult)
         ts(V("ID16"), V("ID"), 16.0, O.mult)
         ts(V("SD"), V("S1"), lane, O.mult)
@@ -335,33 +346,39 @@ def rank_program(g, core, T, topo):
     fill(C(17), 1.0)
     fill(V("SV", 9, 12), float(EMPTY * SL))
 
-    def dot(out, a, k):
-        tt(w_(k, 3), a, EE, O.mult)
-        red(out, w_(k, 3), O.add)
-
-    def split(o, buf, x):
-        p = V("PN", o * 8, o * 8 + 8)
-        ts(V(buf, x, x + 8), p, MAGIC, O.add, MAGIC, O.subtract)
-        tt(V(buf, x + 8, x + 16), p, V(buf, x, x + 8), O.subtract)
+    def split(blocks):
+        for o, (buf, x) in blocks:
+            ts(V(buf, x, x + 8), V("PN", o * 8, o * 8 + 8), MAGIC, O.add, MAGIC, O.subtract)
+        for o, (buf, x) in blocks:
+            tt(V(buf, x + 8, x + 16), V("PN", o * 8, o * 8 + 8), V(buf, x, x + 8), O.subtract)
 
     mm(V("PN", 0, 32), [(V("B8", 15 - i, 143 - i, P=8), V("F8", i, 512, 16, P=8)) for i in range(16)])
-    for q in range(4):
-        split(q, "A", q * 144 + 128)
-    dot(BASE, PT, 0)
+    split([(q, ("A", q * 144 + 128)) for q in range(4)])
 
     def parents(r):
         if r:
             level_a(r - 1)
-            dot(BASE, PT, 0)
+        tt(w_(0, 3), PT, EE, O.mult)
+        red(BASE, w_(0, 3), O.add)
         ts(V("OFA"), V("CL"), BASE, O.add)
+        tt(w_(3, 3), V("E8C", 0, 3), EE, O.mult)
+        tt(w_(23, 3), V("SV", 3, 6), EE, O.mult)
+        red(E8, w_(3, 3), O.add)
+        red(THR, w_(23, 3), O.add)
+        if r:
+            level_b()
+        tt(w_(6, 3), LO, EE, O.mult)
+        ts(THR, THR, -1023.0, O.add, 1.0 / 32, O.mult)
+        red(LOE, w_(6, 3), O.add)
+        fill(V("TT"), 511.5)
+        ts(CC, LOE, -4096.0, O.mult, 444.0 + 4096.0 * 1023, O.add)
+        ts(LIM, LOE, -1.0, O.mult, 1022.5, O.add)
+        ts(LMN, LOE, -1023.0, O.add)
         lay = V("A", 0, (r + 1) * SL)
         cp(V("S", 0, 256), IND(lay, V("OFA", 0, 16)))
         act(V("S", 256, 512), IND(lay, V("OFA", 16, 32)), F.Copy)
         act(V("FS"), IND(lay, V("OFA", 32, 40)), F.Copy)
         mm(V("PU", 0, 32), wraps("WM", "S"))
-        dot(E8, V("E8C", 0, 3), 3)
-        dot(THR, V("SV", 3, 6), 9)
-        ts(THR, THR, -1023.0, O.add, 1.0 / 32, O.mult)
         tt(V("T8"), V("FS", 0, 64), V("FS", 64, 128), O.add)
         ts(V("P8"), V("T8"), THR, O.is_ge, 32.0, O.mult)
         tt(V("FS", 0, 64), V("FS", 0, 64), V("P8"), O.add)
@@ -426,10 +443,12 @@ def rank_program(g, core, T, topo):
         parents(r)
         cp(V("UI"), V("PU", 0, 32))
         ts(V("UU"), V("UI"), 4095, O.bitwise_and)
-        cp(V("UF"), V("UU"))
         tt(V("USQ"), V("UU"), V("UU"), O.mult)
+        cp(V("UF"), V("UU"))
         ts(V("BB"), V("USQ"), 4, O.arith_shift_right)
-        for j in range(8):
+        for j in range(2):
+            ts(V("TJ", j * 32, j * 32 + 32), V("UU"), float(KA[j]), O.mult, E8, O.add)
+        for j in range(2, 8):
             act(V("TJ", j * 32, j * 32 + 32), V("UF"), F.Identity, bias=E8, scale=float(KA[j]))
 
         def numbers(j0, j1):
@@ -453,8 +472,8 @@ def rank_program(g, core, T, topo):
             act(V("CH", x, y), V("PC%d" % (k // 2), 0, 512) if k in (1, 3) else V("D", x, y), F.Abs)
 
         def sums(k):
-            mm(V("PX" if k < 2 else "PEA", k * 64, k * 64 + 64), [(V("IDF"), V("FS", 0, 64)), (V("IDF"), V("FS", 64, 128))]
-               + wraps("XB", "CH", 1024, k * 1024))
+            mm2(V("PX" if k < 2 else "PEA", k * 64, k * 64 + 64), [(V("IDF"), V("FS", 0, 64)), (V("IDF"), V("FS", 64, 128))],
+                wraps("XB", "CH", 1024, k * 1024))
 
         numbers(0, 2)
         other(1)
@@ -473,48 +492,52 @@ def rank_program(g, core, T, topo):
             size(k)
             if k % 2:
                 sums(k // 2)
-        if r:
-            level_b()
-        dot(LOE, LO, 6)
-        ts(CC, LOE, -4096.0, O.mult, 444.0 + 4096.0 * 1023, O.add)
-        ts(LIM, LOE, -1.0, O.mult, 1022.5, O.add)
-        ts(LMN, LOE, -1023.0, O.add)
         if not r:
             consts2()
-        fill(V("TT"), 511.5)
         for p, a, b in (("PX", 0, 128), ("PEA", 128, 256)):
             ts(V("XI", a, b), V(p, a, b), CC, O.add)
             ts(V("OW", a, b), V("XI", a, b), 3, O.bitwise_and)
             ts(V("Y", a, b), V("XI", a, b), 12, O.arith_shift_right, 4095, O.bitwise_and)
             ts(V("OW4", a, b), V("OW", a, b), 8192.0, O.mult)
             tt(V("Z", a, b), V("Y", a, b), V("OW4", a, b), O.add)
-        for o in (2, 0, 1):
-            act(V("X", o * 256, o * 256 + 256), V("Z"), F.Abs, bias=V("BO", o, o + 1))
-        ts(V("OW3"), V("OW"), 3.0, O.not_equal, 8192.0, O.mult)
-        tt(V("XH", 256, 512), V("OW3"), V("Y"), O.add)
-        cp(V("XH", 0, 256), V("X", 512, 768))
+            for o in (0, 1, 2):
+                act(V("X", o * 256 + a, o * 256 + b), V("Z", a, b), F.Abs, bias=V("BO", o, o + 1))
+            ts(V("OW3", a, b), V("OW", a, b), 3.0, O.not_equal, 8192.0, O.mult)
+            tt(V("XH", 768 + a, 768 + b), V("OW3", a, b), V("Y", a, b), O.add)
+            if not a:
+                cp(V("XH", 512, 640), V("X", 512, 640))
+        cp(V("XH", 640, 768), V("X", 640, 768))
+        for k in range(2):
+            mm(V("PC%d" % k, 64, 66), [(V("ID"), V("CQ"))])
         s = 512
         while s:
+            mm(V("PN", 0, 2), [(V("BLK"), V("CA"))], True, False)
             for o in (0, 1):
                 act(V("DA", o * 256, o * 256 + 256), V("X", o * 256, o * 256 + 256), F.Sign, bias=V("TT", o, o + 1), scale=-1.0, acc=V("CN", o, o + 1))
             for o in (3, 2):
                 z = o * 256 - 512
-                ts(V("DV", z, z + 256), V("XH", z, z + 256), V("TT", o, o + 1), O.is_lt)
-                mm(V("PC%d" % (o - 2), 0, 64), [(V("BLK"), V("DV", z + 64 * x, z + 64 * x + 64)) for x in range(4)])
-            mm(V("PN", 0, 2), [(V("BLKF"), V("CN", 0, 2))])
-            ts(V("TTH"), V("TT"), -s / 2.0 if s > 1 else -1.0, O.add)
+                ts(V("DV", z, z + 256), V("XH", z + 512, z + 768), V("TT", o, o + 1), O.is_lt)
+                mm(V("PC%d" % (o - 2), 0, 64), [(V("NB"), V("DV", z + 64 * x, z + 64 * x + 64)) for x in range(4)])
+            mm(V("PN", 0, 2), [(V("NBF"), V("CN", 0, 2))], False, True)
+            if s > 1:
+                ts(V("TLO"), V("TT"), -s / 2.0, O.add)
+                ts(V("THI"), V("TT"), s / 2.0, O.add)
+            else:
+                ts(V("TLO"), V("TT"), -1.0, O.add, LIM, O.min)
+                ts(V("THI"), V("TT"), LIM, O.min)
+            if s in (256, 128):
+                o = s // 128 - 1
+                cp(V("XH", o * 256, o * 256 + 256), V("X", o * 256, o * 256 + 256))
             for o in (3, 2):
-                red(V("CN", o, o + 1), V("PC%d" % (o - 2), 0, 64), O.add)
-            ts(V("TU", 2, 4), V("CN", 2, 4), 128.5, O.is_le, float(s), O.mult)
-            tt(V("TT", 2, 4), V("TTH", 2, 4), V("TU", 2, 4), O.add)
-            ts(V("TU", 0, 2), V("PN", 0, 2), -3839.5, O.is_le, float(s), O.mult)
-            tt(V("TT", 0, 2), V("TTH", 0, 2), V("TU", 0, 2), O.add)
+                red(V("QN", o, o + 1), V("PC%d" % (o - 2), 0, 66), O.add)
+            for o in (3, 2, 0, 1):
+                ts(V("TT", o, o + 1), V("PN", o, o + 1) if o < 2 else V("QN", o, o + 1), V("TLO", o, o + 1), O.max, V("THI", o, o + 1), O.min)
             s //= 2
-        ts(V("TTH"), V("TT"), LIM, O.min)
-        for o in (2, 3, 0, 1):
-            ts(V("KP", o * 256, o * 256 + 256), V("X", o * 256, o * 256 + 256) if o < 2 else V("XH", o * 256 - 512, o * 256 - 256), V("TTH", o, o + 1), O.is_lt)
-        for o in (2, 3, 0, 1):
-            scan(V("R", o * 256, o * 256 + 256), V("KP", o * 256, o * 256 + 256), V("ZERO"), O.add, O.add)
+        for p in ((2, 3), (0, 1)):
+            for o in p:
+                ts(V("KP", o * 256, o * 256 + 256), V("XH", o * 256, o * 256 + 256), V("TT", o, o + 1), O.is_lt)
+            for o in p:
+                scan(V("R", o * 256, o * 256 + 256), V("KP", o * 256, o * 256 + 256), V("ZERO"), O.add, O.add)
 
         def places(o):
             mm(V("PC%d" % (o // 2), o % 2 * 256, o % 2 * 256 + 256), [(V("BLK"), V("R", o * 256, o * 256 + 256)), (V("NUT"), V("KP", o * 256, o * 256 + 256))])
@@ -530,22 +553,22 @@ def rank_program(g, core, T, topo):
             red(V("EA", o, o + 1), V("EM", o * 16, o * 16 + 16), O.add)
         for o in range(4):
             ts(V("IA", o * 128, o * 128 + 128), V("K", 0, 128), V("EA", o, o + 1), O.is_ge)
-        mm(V("PL", 0, 32), [(V("ID"), V("O32"))] + wraps("S1", "IA"))
+        mm2(V("PL", 0, 32), [(V("ID"), V("O32"))], wraps("S1", "IA"))
         for o in range(4):
             act(V("EBW", o * 32, o * 32 + 16), V("PEB", o * 16, o * 16 + 16), F.Copy)
         mb = r * 16 + me * 4
-        red(w_(61), V("TTH"), O.min)
+        red(w_(61), V("TT"), O.min)
         red(w_(60), V("Y"), O.min)
         ts(V("MB", mb, mb + 1), w_(61), LOE, O.add, 0.5, O.add)
         ts(V("MB", mb + 1, mb + 2), w_(60), LOE, O.add, 1023.0, O.min)
-        send(r, "b", "MB", ("MB", mb, mb + 2), {d: (mb, mb + 2) for d in hop})
-        arrive(r, "b", "MB", [(r * 16 + q * 4, r * 16 + q * 4 + 2) for q in range(4) if q != me])
+        send(r, "b", "MB", ("MB", mb), {d: mb for d in hop}, 2)
+        arrive(r, "b", "MB", r * 16, 4, 2)
         ts(V("YW", 0, 256), V("Y"), LMN, O.add)
         cp(V("OFB"), V("PL", 0, 32))
         tt(V("AB", 0, 32), V("PL", 0, 32), V("O32"), O.subtract)
         places(3)
         tt(V("IB"), IND(V("EBW"), V("OFB")), V("K"), O.is_le)
-        mm(V("PL", 0, 32), [(V("ID"), V("O272")), (V("ID16"), V("AB", 0, 32))] + wraps("S1", "IB"))
+        mm2(V("PL", 0, 32), [(V("ID"), V("O272")), (V("ID16"), V("AB", 0, 32))], wraps("S1", "IB"))
         places(0)
         places(1)
         heads(2)
@@ -558,30 +581,24 @@ def rank_program(g, core, T, topo):
         heads(0)
         heads(1)
         tt(V("OH", 0, 256), IND(V("W", 0, 544), V("OFW", 0, 16)), V("K1", 0, 256), O.is_equal)
-        mm(V("PU", 0, 32), [(V("ID16"), V("CB"))] + wraps("SD", "OH"))
+        mm2(V("PU", 0, 32), [(V("ID16"), V("CB"))], wraps("SD", "OH"))
         tt(V("CG", 0, 512), IND(V("YW"), V("OFC")), V("OH", 0, 512), O.mult)
         mm(V("PN", 0, 32), wraps("S32", "CG"))
         cp(V("OFN"), V("PU", 0, 32))
-        blk = {}
-        for o in range(4):
-            blk[T.cores[o]] = ("A", (r + 1) * SL + me * 144) if o == me else ("SND", r * SL + o * 144)
-        far = [d for d in hop] + [core]
-        for k, d in enumerate(far):
-            n, x = blk[d]
-            o = T.cores.index(d)
-            v = IND(V("CH"), V("OFN", o * 8, o * 8 + 8))
+        order = [T.cores.index(d) for d in hop] + [me]
+        blk = {o: ("SND", r * SL + o * 144) for o in order}
+        blk[me] = ("A", (r + 1) * SL + me * 144)
+        for k, o in enumerate(order):
+            out, v = V(blk[o][0], blk[o][1], blk[o][1] + 128), IND(V("CH"), V("OFN", o * 8, o * 8 + 8))
             if k == 1:
-                cp(V(n, x, x + 128), v)
+                cp(out, v)
             else:
-                act(V(n, x, x + 128), v, F.Copy)
+                act(out, v, F.Copy)
         pre(r)
-        for d in far:
-            n, x = blk[d]
-            split(T.cores.index(d), n, x + 128)
-            if d == far[2]:
-                x = (r + 1) * SL + me * 144
-                send(r, "a", "SND", ("A", x, x + 144), {d: (blk[d][1], blk[d][1] + 144) for d in hop})
-        arrive(r, "a", "A", [((r + 1) * SL + q * 144, (r + 1) * SL + q * 144 + 144) for q in range(4) if q != me])
+        split([(o, (blk[o][0], blk[o][1] + 128)) for o in order[:3]])
+        send(r, "a", "SND", ("A", (r + 1) * SL + me * 144), {d: blk[T.cores.index(d)][1] for d in hop}, 144)
+        split([(me, (blk[me][0], blk[me][1] + 128))])
+        arrive(r, "a", "A", (r + 1) * SL, 144, 144)
         if not r:
             consts3()
 
@@ -612,7 +629,7 @@ def rank_program(g, core, T, topo):
     ts(V("EA"), V("EA"), V("LC", 5, 6), O.add)
     for k in range(12):
         ts(V("IA", k * 128, k * 128 + 128), V("K", 0, 128), V("EA", k, k + 1), O.is_ge)
-    mm(V("PL", 0, 96), [(V("ID"), V("B8C"))] + wraps("S1", "IA", 1536))
+    mm2(V("PL", 0, 96), [(V("ID"), V("B8C"))], wraps("S1", "IA", 1536))
     tt(V("W3"), V("PC0", 0, 96), V("KP3"), O.mult)
     level_b()
     cp(V("YT", 0, 3), LO)
@@ -626,7 +643,7 @@ def rank_program(g, core, T, topo):
     for l in range(3):
         a, b = l * 512, l * 512 + 512
         tt(V("OH", a, b), IND(V("W3"), V("OF3", l * 32, l * 32 + 32)), V("K1"), O.is_equal)
-    mm(V("PU", 0, 96), [(V("ID16"), V("AB")), (V("ID"), V("B256"))] + wraps("SE", "OH", 1536))
+    mm2(V("PU", 0, 96), [(V("ID16"), V("AB")), (V("ID"), V("B256"))], wraps("SE", "OH", 1536))
     cp(V("YT8", P=8), V("PX", 0, 8, P=8))
     dma("Y", EXT(T.yt[:, :]), V("YT8", P=8), "o0")
 

from concourse.bass import DstId, RemoteDMATransfer
from concourse.mybir import AluOpType as O, AxisListType, ActivationFunctionType as F

NR = 8
SL = 576
EMPTY = 9
WT = [1, 3, 7, 13, 21, 35, 49, 67, 85, 107, 129, 155, 181, 211, 241, 253]
KA = [17, 101, 263, 389, 547, 701, 859, 1021]
MAGIC = float(3 << 22)

_f, _b, _h, _i, _u = "float32", "bfloat16", "float16", "int32", "uint16"
PSUM = ("PU", "PX", "PN", "PC0", "PC1", "PEA", "PEB", "PL")
SCRATCH = {}
for _n, _w, _d in (
        ("A", 10 * SL, _b), ("OPW", 4096, _b), ("SND", NR * SL, _b), ("MB", NR * 16, _f), ("S", 512, _b), ("FS", 128, _b), ("D", 4096, _b),
        ("GA", 1024, _b), ("CH", 4112, _b), ("OFA", 40, _u), ("OFO", 256, _u), ("OFB", 32, _u), ("OFW", 32, _u), ("OFV", 16, _u),
        ("OFC", 32, _u), ("OFN", 32, _u), ("UI", 32, _i), ("UU", 32, _i), ("UF", 32, _f), ("USQ", 32, _i), ("BB", 32, _i),
        ("TJ", 256, _f), ("VJ", 256, _i), ("VK", 256, _i), ("XI", 256, _i), ("Y", 256, _i), ("OW", 256, _i), ("OW3", 256, _f), ("OW4", 256, _f),
        ("Z", 256, _f), ("YW", 272, _f), ("X", 768, _f), ("XH", 1024, _h), ("DA", 512, _b), ("DV", 512, _b), ("KP", 1024, _b), ("R", 1024, _b),
        ("W", 1088, _b), ("IA", 1536, _b), ("IB", 512, _b), ("OH", 1536, _b), ("CG", 1536, _h), ("EBW", 128, _b), ("AB", 96, _b), ("CB", 32, _b),
        ("EM", 96, _f), ("EA", 12, _f), ("T8", 64, _f), ("P8", 64, _f), ("TT", 4, _f), ("TLO", 4, _f), ("THI", 4, _f), ("CN", 4, _f), ("QN", 4, _f),
        ("SV", 64, _f), ("SW", 64, _f), ("MD", 16, _f),
        ("ONE", 256, _b), ("ZERO", 256, _b), ("BLK", 128, _b), ("BLKF", 128, _f), ("NBF", 128, _f), ("NB", 128, _b), ("CQ", 2, _b), ("CA", 2, _b),
        ("NUT", 128, _b), ("ID", 128, _b), ("IDN", 128, _b), ("IDF", 128, _b), ("ID16", 128, _b), ("S1", 144, _b), ("SD", 144, _b), ("SE", 144, _b),
        ("S32", 144, _h), ("WM", 144, _b), ("XB", 144, _h), ("K", 512, _b), ("K1", 512, _b), ("CL", 40, _f), ("O32", 32, _b), ("O272", 32, _b),
        ("DM", 64, _f), ("LM", 16, _f), ("WR", 16, _f), ("W2", 16, _f), ("LC", 16, _f), ("LI", 8, _i), ("BO", 4, _f), ("E8C", 4, _f),
        ("G8", 8, _h), ("G8F", 8, _f),
        ("S3", 3072, _b), ("FF", 384, _b), ("F3", 96, _f), ("KP3", 96, _b), ("R3", 96, _b), ("RM", 96, _b), ("W3", 96, _b),
        ("OF3", 96, _u), ("OG3", 120, _u), ("OP3", 96, _u), ("B8C", 96, _b), ("B256", 96, _b), ("DM3", 96, _f), ("YL", 1536, _b), ("YT", 8, _f)):
    SCRATCH[_n] = ("sbuf", [128, _w], _d)
for _n, _w, _d in (("B8", 144, _h), ("F8I", 512, _i), ("F8", 512, _h), ("YF", 1536, _f), ("YT8", 8, _f)):
    SCRATCH[_n] = ("sbuf", [8, _w], _d)
for _n in PSUM:
    SCRATCH[_n] = ("psum", [128, 512], _f)
SEMAPHORES = (["sV", "sS", "sT", "sG", "ls"] + ["%s%d" % (s, r) for s in "ab" for r in range(NR)]
              + ["l%d" % k for k in range(9)] + ["o%d" % k for k in range(5)])


def ways(core, T, topo):
    hop, used = {}, []
    for d in T.cores:
        if d == core:
            continue
        if topo.may_write(core, d):
            hop[d] = d
        else:
            c = [x for x in topo.cores_of(core) if x != core and x not in used and topo.die(x) == topo.die(core) and topo.may_write(x, d)]
            hop[d] = c[0]
            used.append(c[0])
    return hop


def bits(es):
    m = 0
    for e in es:
        m |= 1 << e
    return m


def hop_engines(core, hop, topo, s):
    far = [d for d in hop if hop[d] != d]
    res = {d: topo.engines(core, d) for d in hop if hop[d] == d}
    used = [] if s == "a" else [e for d in res for e in res[d]]
    for k, d in enumerate(far):
        rest = [e for e in topo.engines(core, hop[d]) if e not in used]
        n = len(rest) // len(far)
        res[d] = rest[k * n:(k + 1) * n]
    return res


def relay(g, core, T, topo):
    local = 0
    for q, rk in enumerate(T.cores):
        hop = ways(rk, T, topo)
        for d in hop:
            if hop[d] != core or d == core:
                continue
            rid, pid = topo.addr(d, core)
            m = topo.mask(core, d)
            for r in range(NR):
                for s, buf, x, w in (("b", T.MB, r * 16 + q * 4, 2), ("a", T.A, (r + 1) * SL + q * 144, 144)):
                    sem = T.sem["%s%d" % (s, r)]
                    g.wait_ge(sem, len(hop_engines(rk, hop, topo, s)[d]))
                    g.remote_dma(buf[:, x:x + w], buf[:, x:x + w], sem, T.sem.ls, pid, rid, m)
                    local += len(topo.engines(core, d))
    if local:
        g.wait_ge(T.sem.ls, local)


def rank_program(g, core, T, topo):
    me = T.rank_of(core)
    if me is None:
        relay(g, core, T, topo)
        return
    hop = ways(core, T, topo)
    queue = {"V": g.vector, "S": g.scalar, "T": g.tensor, "G": g, "Y": g.sync}
    count = {"V": 0, "S": 0, "T": 0, "G": 0, "ls": 0}
    known = {q: {} for q in queue}
    logs = {}

    def V(name, a=None, b=None, s=1, P=128):
        t = T[name]
        if a is None:
            a, b = 0, t.shape[-1]
        ap = t[0:P, a:b:s] if s != 1 else t[0:P, a:b]
        return {"ap": ap, "r": [(name, 0, 512) if name in PSUM else (name, a, b)]}

    def IND(w, o):
        return {"ap": w["ap"].indirect(o["ap"]), "r": w["r"] + o["r"]}

    def begin(e, outs, ins):
        recs = {}
        for views, wr in ((ins, False), (outs, True)):
            for v in views:
                for n, a, b in v["r"]:
                    for (x, y, w, e2, sem, val, clk) in logs.get(n, []):
                        if x < b and a < y and (wr or w):
                            if sem not in recs or recs[sem][1] < val:
                                recs[sem] = (sem, val, clk)
        k = known[e]
        for sem, val, clk in sorted(recs.values(), key=lambda z: -len(z[2])):
            if k.get(sem, 0) < val:
                queue[e].wait_ge(T.sem[sem], val)
                k[sem] = val
                for x in clk:
                    if k.get(x, 0) < clk[x]:
                        k[x] = clk[x]

    def done(e, clk, sem, val, outs, ins):
        clk = dict(clk)
        clk[sem] = val
        for views, wr in ((ins, False), (outs, True)):
            for v in views:
                for n, a, b in v["r"]:
                    old = logs.get(n, [])
                    if wr:
                        old = [z for z in old if not (a <= z[0] and z[1] <= b)]
                    else:
                        old = [z for z in old if z[2] or z[3] != e or not (a <= z[0] and z[1] <= b)]
                    logs[n] = old + [(a, b, wr, e, sem, val, clk)]

    def op(e, outs, ins, call):
        begin(e, outs, ins)
        count[e] += 1
        call(queue[e]).then_inc(T.sem["s" + e], 1)
        done(e, known[e], "s" + e, count[e], outs, ins)

    def dma(e, out, in_, sem):
        begin(e, [out], [in_])
        queue[e].dma_start(out["ap"], in_["ap"]).then_inc(T.sem[sem], 16)
        done("dma" + sem, {}, sem, 16, [out], [in_])

    def EXT(ap):
        return {"ap": ap, "r": []}

    def val(s):
        return s["ap"] if isinstance(s, dict) else s

    def vs(*a):
        return [x for x in a if isinstance(x, dict)]

    def ts(out, a, s1, op0, s2=None, op1=None):
        if op1 is None:
            op("V", [out], vs(a, s1), lambda q: q.tensor_scalar(out["ap"], a["ap"], val(s1), None, op0))
        else:
            op("V", [out], vs(a, s1, s2), lambda q: q.tensor_scalar(out["ap"], a["ap"], val(s1), val(s2), op0, op1))

    def tt(out, a, b, o):
        op("V", [out], [a, b], lambda q: q.tensor_tensor(out["ap"], a["ap"], b["ap"], o))

    def cp(out, a):
        op("V", [out], [a], lambda q: q.tensor_copy(out["ap"], a["ap"]))

    def red(out, a, o):
        op("V", [out], [a], lambda q: q.tensor_reduce(out["ap"], a["ap"], AxisListType.X, o))

    def fill(out, c):
        op("V", [out], [], lambda q: q.memset(out["ap"], c))

    def scan(out, a, z, op0, op1):
        op("V", [out], [a, z], lambda q: q.tensor_tensor_scan(out["ap"], a["ap"], z["ap"], 0.0, op0, op1))

    def act(out, a, f, bias=None, scale=None, acc=None):
        kw = {}
        if bias is not None:
            kw["bias"] = val(bias)
        if scale is not None:
            kw["scale"] = scale
        if acc is not None:
            kw["accum_out"] = acc["ap"]
        op("S", vs(out, acc), vs(a, bias), lambda q: q.activation(out["ap"], a["ap"], f, **kw))

    def mm(out, pairs, start=True, stop=True):
        n = len(pairs)

        def call(q):
            x = None
            for k, (l, r) in enumerate(pairs):
                x = q.matmul(out["ap"], l["ap"], r["ap"], start and k == 0, stop and k == n - 1)
            return x
        op("T", [out], [v for p in pairs for v in p], call)

    def mm2(out, early, late):
        mm(out, early, True, False)
        mm(out, late, False, True)

    def iota(out, pattern, base, cm):
        op("G", [out], [], lambda q: q.iota(out["ap"], pattern, base, cm, allow_small_or_imprecise_dtypes=True))

    def sel(out, a, pattern, cmp_, base, cm):
        op("G", [out], [a], lambda q: q.affine_select(out["ap"], a["ap"], pattern, cmp_, 0.0, base, cm))

    def wrap(base, buf, i, w=512, x=0):
        return (V(base, 15 - i, 143 - i), V(buf, x + i, x + w, 16))

    def wraps(base, buf, w=512, x=0):
        return [wrap(base, buf, i, w, x) for i in range(16)]

    def send(r, s, src, dst, w, width):
        begin("G", [], [V(src, w[d], w[d] + width) for d in hop])
        eng = hop_engines(core, hop, topo, s)
        far, near = [d for d in hop if hop[d] != d], [d for d in hop if hop[d] == d]
        for ds in ([far, near] if s == "a" else [far + near]):
            tr = []
            for d in ds:
                rid, pid = topo.addr(hop[d], core)
                tr.append(RemoteDMATransfer(dst_ids=[DstId(rid=rid, pnc=pid)], dma_engine_mask=bits(eng[d]), remote_sem=T.sem["%s%d" % (s, r)],
                                            src=T[src][:, w[d]:w[d] + width], dst=T[dst[0]][:, dst[1]:dst[1] + width]))
                count["ls"] += len(eng[d])
            g.remote_dma_fused(tr, local_sem=T.sem.ls)

    def arrive(r, s, name, x, stride, width):
        n = 0
        for c in T.cores:
            if c != core:
                h = ways(c, T, topo)
                n += len(hop_engines(c, h, topo, s)[core]) if h[core] == core else len(topo.engines(h[core], core))
        sem = "%s%d" % (s, r)
        for q in range(4):
            if q != me:
                logs[name] = logs.get(name, []) + [(x + q * stride, x + q * stride + width, True, "net", sem, n, {sem: n})]

    dma("Y", V("F8I", P=8), EXT(T.f0[:, :]), "l0")
    for q in range(4):
        dma("Y" if q % 2 else "S", V("A", q * 144, q * 144 + 128), EXT(T.s0[:, q * 128:q * 128 + 128]), "l%d" % (1 + q))
    for q in range(4):
        dma("S" if q % 2 else "Y", V("OPW", q * 1024, q * 1024 + 1024), EXT(T.opr[:, q * 1024:q * 1024 + 1024]), "l%d" % (5 + q))

    fill(V("ONE"), 1.0)
    iota(V("LI", 0, 1), [[1, 1]], 0, 1)
    iota(V("LM"), [[1, 16]], 0, 0)
    iota(V("CL", 0, 32), [[144, 4], [16, 8]], 0, 0)
    iota(V("CL", 32, 40), [[8, 2], [0, 2], [288, 2]], 128, 0)
    sel(V("S1"), V("ONE", 0, 144), [[0, 9], [1, 16]], O.is_equal, -15, 0)
    sel(V("S1"), V("S1"), [[-16, 9], [0, 16]], O.is_ge, 0, 1)
    sel(V("S1"), V("S1"), [[16, 9], [0, 16]], O.is_ge, 15, -1)
    sel(V("B8", P=8), V("ONE", 0, 144, P=8), [[0, 9], [1, 16]], O.is_equal, -15, 0)
    sel(V("B8", P=8), V("B8", P=8), [[1, 9], [0, 16]], O.is_equal, 0, -1)
    sel(V("ID"), V("ONE", 0, 128), [[-1, 128]], O.is_equal, 0, 1)
    sel(V("BLK"), V("ONE", 0, 128), [[-16, 8], [0, 16]], O.is_ge, 0, 1)
    sel(V("BLK"), V("BLK"), [[16, 8], [0, 16]], O.is_ge, 15, -1)
    sel(V("NUT"), V("BLK"), [[-1, 128]], O.is_gt, 0, 1)
    iota(V("DM"), [[0, 4], [1, 16]], 0, 0)
    iota(V("K"), [[0, 4], [1, 128]], 0, 0)
    iota(V("O32"), [[32, 4], [0, 8]], 0, 0)
    iota(V("O272"), [[272, 4], [0, 8]], 0, 0)
    iota(V("K1"), [[0, 4], [1, 128]], 1, 0)
    iota(V("B8C"), [[8, 12], [0, 8]], 0, 0)
    iota(V("B256"), [[256, 12], [0, 8]], 128, 0)
    iota(V("DM3"), [[0, 12], [1, 8]], 0, 0)
    sel(V("G8"), V("ONE", 0, 8), [[-16, 8]], O.is_ge, 0, 1)
    sel(V("G8"), V("G8"), [[16, 8]], O.is_ge, 15, -1)
    for i in range(16):
        fill(V("WR", i, i + 1), float(WT[i]))
    for o in range(3):
        fill(V("E8C", o, o + 1), 811.0 * o)
    ts(V("LI", 1, 2), V("LI", 0, 1), 15, O.bitwise_and)
    lane = V("LC", 0, 1)
    cp(lane, V("LI", 1, 2))
    ts(V("LI", 2, 3), V("LI", 1, 2), 7, O.bitwise_and)
    ts(V("LI", 3, 4), V("LI", 1, 2), 3, O.arith_shift_right)
    ts(V("LM"), V("LM"), lane, O.is_equal)
    ts(V("LC", 3, 4), V("LI", 3, 4), 144.0, O.mult)
    tt(V("W2"), V("WR"), V("LM"), O.mult)
    tt(V("LC", 4, 5), V("LC", 3, 4), V("LI", 2, 3), O.add)
    red(V("LC", 1, 2), V("W2"), O.add)
    ts(V("CL", 0, 32), V("CL", 0, 32), lane, O.add)
    ts(V("CL", 32, 40), V("CL", 32, 40), V("LC", 4, 5), O.add)
    cp(V("LI", 4, 5), V("LC", 1, 2))
    ts(V("LI", 5, 6), V("LI", 4, 5), 3, O.bitwise_and)
    ts(V("LC", 2, 3), V("LI", 5, 6), -1.0, O.mult, 1026.0, O.add)
    ts(V("WM"), V("S1"), V("LC", 1, 2), O.mult)
    ts(V("F8", P=8), V("F8I", P=8), -1023.0, O.add)
    ts(V("B8", P=8), V("B8", P=8), 1.0 / 32, O.mult)

    def consts1():
        ts(V("XB"), V("S1"), V("LC", 2, 3), O.mult)
        ts(V("IDF"), V("ID"), 131072.0, O.mult)
        ts(V("IDN"), V("ID"), -1.0, O.mult)
        for o in range(4):
            fill(V("BO", o, o + 1), -8192.0 * o)
        fill(V("CH", 4096, 4112), 0.0)

    def consts2():
        cp(V("BLKF"), V("BLK"))
        ts(V("NBF"), V("BLK"), -4096.0, O.mult)
        ts(V("NB"), V("BLK"), -4096.0, O.mult)
        fill(V("CQ", 0, 1), 524288.0)
        fill(V("CQ", 1, 2), 2048.0)
        ts(V("LC", 8, 9), lane, 0.0, O.is_equal, -15728640.0, O.mult)
        ts(V("LC", 9, 10), lane, 1.0, O.is_equal, 4096.0, O.mult)
        for o in range(2):
            tt(V("CA", o, o + 1), V("LC", 8, 9), V("LC", 9, 10), O.add)
        ts(V("NUT"), V("NUT"), -1.0, O.mult)
        ts(V("ID16"), V("ID"), 16.0, O.mult)
        ts(V("SD"), V("S1"), lane, O.mult)
        ts(V("S32"), V("S1"), 1.0 / 32, O.mult)
        ts(V("DM"), V("DM"), lane, O.is_equal)
        fill(V("ZERO"), 0.0)
        fill(V("YW", 256, 272), 0.0)
        fill(V("W"), 0.0)
        fill(V("EBW"), 1000.0)

    def consts3():
        fill(V("A", EMPTY * SL, EMPTY * SL + SL), 0.0)
        ts(V("LC", 6, 7), lane, -128.0, O.add)
        ts(V("RM"), V("DM3"), 0.0, O.is_gt)
        ts(V("DM3"), V("DM3"), lane, O.is_equal)
        ts(V("LC", 5, 6), lane, 6.5, O.is_gt, 1000.0, O.mult)
        ts(V("SE"), V("S1"), V("LC", 6, 7), O.mult)
        ts(V("G8F"), V("G8"), 1.0 / 16, O.mult)
        ts(V("G8"), V("G8"), 32.0, O.mult)
        fill(V("S3"), 0.0)

    def C(k):
        return V("SV", k, k + 1)

    def w_(k, n=1):
        return V("SW", k, k + n)

    LO, HI, PT, U, EE, EL, ER = V("SV", 0, 3), V("SV", 4, 7), V("SV", 8, 11), C(12), V("SV", 17, 20), V("SV", 18, 21), V("SV", 16, 19)
    LOE, BASE, E8, CC, LIM, LMN, THR = C(24), C(25), C(26), C(27), C(28), C(29), C(30)
    fill(V("SV"), 0.0)
    fill(U, 1023.0)
    fill(C(3), 100000.0)
    fill(C(17), 1.0)
    fill(V("SV", 9, 12), float(EMPTY * SL))

    def split(blocks):
        for o, (buf, x) in blocks:
            ts(V(buf, x, x + 8), V("PN", o * 8, o * 8 + 8), MAGIC, O.add, MAGIC, O.subtract)
        for o, (buf, x) in blocks:
            tt(V(buf, x + 8, x + 16), V("PN", o * 8, o * 8 + 8), V(buf, x, x + 8), O.subtract)

    mm(V("PN", 0, 32), [(V("B8", 15 - i, 143 - i, P=8), V("F8", i, 512, 16, P=8)) for i in range(16)])
    split([(q, ("A", q * 144 + 128)) for q in range(4)])

    def parents(r):
        if r:
            level_a(r - 1)
        tt(w_(0, 3), PT, EE, O.mult)
        red(BASE, w_(0, 3), O.add)
        ts(V("OFA"), V("CL"), BASE, O.add)
        tt(w_(3, 3), V("E8C", 0, 3), EE, O.mult)
        tt(w_(23, 3), V("SV", 3, 6), EE, O.mult)
        red(E8, w_(3, 3), O.add)
        red(THR, w_(23, 3), O.add)
        if r:
            level_b()
        tt(w_(6, 3), LO, EE, O.mult)
        ts(THR, THR, -1023.0, O.add, 1.0 / 32, O.mult)
        red(LOE, w_(6, 3), O.add)
        fill(V("TT"), 511.5)
        ts(CC, LOE, -4096.0, O.mult, 444.0 + 4096.0 * 1023, O.add)
        ts(LIM, LOE, -1.0, O.mult, 1022.5, O.add)
        ts(LMN, LOE, -1023.0, O.add)
        lay = V("A", 0, (r + 1) * SL)
        cp(V("S", 0, 256), IND(lay, V("OFA", 0, 16)))
        act(V("S", 256, 512), IND(lay, V("OFA", 16, 32)), F.Copy)
        act(V("FS"), IND(lay, V("OFA", 32, 40)), F.Copy)
        mm(V("PU", 0, 32), wraps("WM", "S"))
        tt(V("T8"), V("FS", 0, 64), V("FS", 64, 128), O.add)
        ts(V("P8"), V("T8"), THR, O.is_ge, 32.0, O.mult)
        tt(V("FS", 0, 64), V("FS", 0, 64), V("P8"), O.add)
        if not r:
            consts1()
        for k in range(2):
            mm(V("PC%d" % k, 0, 512), [(V("IDN"), V("S"))], True, False)

    def pre(r):
        tt(w_(22, 3), V("SV", 9, 12), EE, O.mult)
        ts(w_(19, 3), EE, float((r + 1) * SL), O.mult)
        ts(w_(13, 3), EE, -1.0, O.mult, 1.0, O.add)
        ts(w_(36), LOE, 1.0, O.add)
        ts(w_(38), C(17), -1.0, O.mult, 1.0, O.add)
        ts(w_(40, 3), LO, 1.0, O.add)
        tt(w_(19, 3), w_(19, 3), w_(22, 3), O.subtract)
        tt(HI, HI, w_(13, 3), O.mult)
        tt(V("SV", 9, 12), V("SV", 9, 12), w_(19, 3), O.add)

    def level_a(r):
        B, m, rt, lp, bk, up, st = [w_(k) for k in (10, 11, 27, 28, 29, 30, 39)]
        red(w_(12), V("MB", r * 16 + 1, r * 16 + 16, 4), O.min)
        red(B, V("MB", r * 16, r * 16 + 16, 4), O.min)
        ts(V("MD"), V("LM"), w_(12), O.mult)
        mm(V("PN", 0, 16), [(V("BLKF"), V("MD"))])
        ts(w_(13, 3), EE, B, O.mult)
        tt(lp, w_(36), B, O.max)
        tt(HI, HI, w_(13, 3), O.add)
        red(m, V("PN", 0, 16), O.min)
        tt(w_(26), m, B, O.is_lt)
        tt(w_(35), m, B, O.is_ge)
        tt(w_(31), w_(26), C(19), O.mult)
        tt(w_(35), w_(35), C(19), O.max)
        ts(w_(32), w_(31), -4000.0, O.mult, 4000.0, O.add)
        tt(w_(33), w_(32), m, O.max)
        tt(U, U, w_(33), O.min)
        tt(w_(34), m, U, O.is_ge)
        tt(w_(37), lp, U, O.is_ge)
        tt(rt, w_(34), w_(35), O.max)
        tt(w_(37), w_(37), w_(38), O.mult)
        ts(up, rt, -1.0, O.mult, 1.0, O.add)
        tt(bk, w_(37), rt, O.mult)
        ts(w_(46, 3), ER, up, O.mult)
        tt(st, rt, bk, O.subtract)
        ts(w_(49, 3), EL, bk, O.mult)
        ts(w_(43, 3), EE, bk, O.mult)
        ts(w_(52, 3), EE, st, O.mult)
        ts(w_(55, 3), EE, st, O.mult, lp, O.mult)
        tt(w_(16, 3), w_(46, 3), w_(49, 3), O.add)
        tt(EE, w_(16, 3), w_(52, 3), O.add)

    def level_b():
        tt(w_(40, 3), w_(40, 3), HI, O.max)
        tt(w_(43, 3), w_(43, 3), EE, O.add)
        ts(w_(43, 3), w_(43, 3), -1.0, O.mult, 1.0, O.add)
        tt(w_(40, 3), w_(40, 3), w_(49, 3), O.mult)
        tt(LO, LO, w_(43, 3), O.mult)
        tt(w_(40, 3), w_(40, 3), w_(55, 3), O.add)
        tt(LO, LO, w_(40, 3), O.add)

    def rnd(r):
        parents(r)
        cp(V("UI"), V("PU", 0, 32))
        ts(V("UU"), V("UI"), 4095, O.bitwise_and)
        tt(V("USQ"), V("UU"), V("UU"), O.mult)
        cp(V("UF"), V("UU"))
        ts(V("BB"), V("USQ"), 4, O.arith_shift_right)
        for j in range(2):
            ts(V("TJ", j * 32, j * 32 + 32), V("UU"), float(KA[j]), O.mult, E8, O.add)
        for j in range(2, 8):
            act(V("TJ", j * 32, j * 32 + 32), V("UF"), F.Identity, bias=E8, scale=float(KA[j]))

        def numbers(j0, j1):
            for j in range(j0, j1):
                tt(V("VJ", j * 32, j * 32 + 32), V("TJ", j * 32, j * 32 + 32), V("BB"), O.add)
            a, b = j0 * 32, j1 * 32
            ts(V("VK", a, b), V("VJ", a, b), 4095, O.bitwise_and)
            cp(V("OFO", a, b), V("VK", a, b))

        def gather(k):
            x, y = k * 512, k * 512 + 512
            tt(V("D", x, y), IND(V("OPW"), V("OFO", k * 32, k * 32 + 32)), V("S"), O.subtract)

        def other(k):
            z = k // 2 * 512
            act(V("GA", z, z + 512), IND(V("OPW"), V("OFO", k * 32, k * 32 + 32)), F.Copy)
            mm(V("PC%d" % (k // 2), 0, 512), [(V("ID"), V("GA", z, z + 512))], False, True)

        def size(k):
            x, y = k * 512, k * 512 + 512
            act(V("CH", x, y), V("PC%d" % (k // 2), 0, 512) if k in (1, 3) else V("D", x, y), F.Abs)

        def sums(k):
            mm2(V("PX" if k < 2 else "PEA", k * 64, k * 64 + 64), [(V("IDF"), V("FS", 0, 64)), (V("IDF"), V("FS", 64, 128))],
                wraps("XB", "CH", 1024, k * 1024))

        numbers(0, 2)
        other(1)
        gather(0)
        size(0)
        size(1)
        sums(0)
        numbers(2, 8)
        other(3)
        for k in (2, 4, 5, 6, 7):
            gather(k)
        size(2)
        size(3)
        sums(1)
        for k in (4, 5, 6, 7):
            size(k)
            if k % 2:
                sums(k // 2)
        if not r:
            consts2()
        for p, a, b in (("PX", 0, 128), ("PEA", 128, 256)):
            ts(V("XI", a, b), V(p, a, b), CC, O.add)
            ts(V("OW", a, b), V("XI", a, b), 3, O.bitwise_and)
            ts(V("Y", a, b), V("XI", a, b), 12, O.arith_shift_right, 4095, O.bitwise_and)
            ts(V("OW4", a, b), V("OW", a, b), 8192.0, O.mult)
            tt(V("Z", a, b), V("Y", a, b), V("OW4", a, b), O.add)
            for o in (0, 1, 2):
                act(V("X", o * 256 + a, o * 256 + b), V("Z", a, b), F.Abs, bias=V("BO", o, o + 1))
            ts(V("OW3", a, b), V("OW", a, b), 3.0, O.not_equal, 8192.0, O.mult)
            tt(V("XH", 768 + a, 768 + b), V("OW3", a, b), V("Y", a, b), O.add)
            if not a:
                cp(V("XH", 512, 640), V("X", 512, 640))
        cp(V("XH", 640, 768), V("X", 640, 768))
        for k in range(2):
            mm(V("PC%d" % k, 64, 66), [(V("ID"), V("CQ"))])
        s = 512
        while s:
            mm(V("PN", 0, 2), [(V("BLK"), V("CA"))], True, False)
            for o in (0, 1):
                act(V("DA", o * 256, o * 256 + 256), V("X", o * 256, o * 256 + 256), F.Sign, bias=V("TT", o, o + 1), scale=-1.0, acc=V("CN", o, o + 1))
            for o in (3, 2):
                z = o * 256 - 512
                ts(V("DV", z, z + 256), V("XH", z + 512, z + 768), V("TT", o, o + 1), O.is_lt)
                mm(V("PC%d" % (o - 2), 0, 64), [(V("NB"), V("DV", z + 64 * x, z + 64 * x + 64)) for x in range(4)])
            mm(V("PN", 0, 2), [(V("NBF"), V("CN", 0, 2))], False, True)
            if s > 1:
                ts(V("TLO"), V("TT"), -s / 2.0, O.add)
                ts(V("THI"), V("TT"), s / 2.0, O.add)
            else:
                ts(V("TLO"), V("TT"), -1.0, O.add, LIM, O.min)
                ts(V("THI"), V("TT"), LIM, O.min)
            if s in (256, 128):
                o = s // 128 - 1
                cp(V("XH", o * 256, o * 256 + 256), V("X", o * 256, o * 256 + 256))
            for o in (3, 2):
                red(V("QN", o, o + 1), V("PC%d" % (o - 2), 0, 66), O.add)
            for o in (3, 2, 0, 1):
                ts(V("TT", o, o + 1), V("PN", o, o + 1) if o < 2 else V("QN", o, o + 1), V("TLO", o, o + 1), O.max, V("THI", o, o + 1), O.min)
            s //= 2
        for p in ((2, 3), (0, 1)):
            for o in p:
                ts(V("KP", o * 256, o * 256 + 256), V("XH", o * 256, o * 256 + 256), V("TT", o, o + 1), O.is_lt)
            for o in p:
                scan(V("R", o * 256, o * 256 + 256), V("KP", o * 256, o * 256 + 256), V("ZERO"), O.add, O.add)

        def places(o):
            mm(V("PC%d" % (o // 2), o % 2 * 256, o % 2 * 256 + 256), [(V("BLK"), V("R", o * 256, o * 256 + 256)), (V("NUT"), V("KP", o * 256, o * 256 + 256))])

        def heads(o):
            tt(V("W", o * 272, o * 272 + 256), V("PC%d" % (o // 2), o % 2 * 256, o % 2 * 256 + 256), V("KP", o * 256, o * 256 + 256), O.mult)

        places(2)
        mm(V("PEA", 0, 64), [(V("BLK"), V("R", 15, 1024, 16))])
        mm(V("PEB", 0, 64), [wrap("S1", "R", b, 1024) for b in range(16)])
        tt(V("EM", 0, 64), V("PEA", 0, 64), V("DM"), O.mult)
        for o in range(4):
            red(V("EA", o, o + 1), V("EM", o * 16, o * 16 + 16), O.add)
        for o in range(4):
            ts(V("IA", o * 128, o * 128 + 128), V("K", 0, 128), V("EA", o, o + 1), O.is_ge)
        mm2(V("PL", 0, 32), [(V("ID"), V("O32"))], wraps("S1", "IA"))
        for o in range(4):
            act(V("EBW", o * 32, o * 32 + 16), V("PEB", o * 16, o * 16 + 16), F.Copy)
        mb = r * 16 + me * 4
        red(w_(61), V("TT"), O.min)
        red(w_(60), V("Y"), O.min)
        ts(V("MB", mb, mb + 1), w_(61), LOE, O.add, 0.5, O.add)
        ts(V("MB", mb + 1, mb + 2), w_(60), LOE, O.add, 1023.0, O.min)
        send(r, "b", "MB", ("MB", mb), {d: mb for d in hop}, 2)
        arrive(r, "b", "MB", r * 16, 4, 2)
        ts(V("YW", 0, 256), V("Y"), LMN, O.add)
        cp(V("OFB"), V("PL", 0, 32))
        tt(V("AB", 0, 32), V("PL", 0, 32), V("O32"), O.subtract)
        places(3)
        tt(V("IB"), IND(V("EBW"), V("OFB")), V("K"), O.is_le)
        mm2(V("PL", 0, 32), [(V("ID"), V("O272")), (V("ID16"), V("AB", 0, 32))], wraps("S1", "IB"))
        places(0)
        places(1)
        heads(2)
        heads(3)
        ts(V("OFV"), V("PL", 16, 32), -544.0, O.add)
        cp(V("OFW", 0, 16), V("PL", 0, 16))
        tt(V("CB"), V("PL", 0, 32), V("O272"), O.subtract)
        cp(V("OFC"), V("CB"))
        tt(V("OH", 256, 512), IND(V("W", 544, 1088), V("OFV")), V("K1", 0, 256), O.is_equal)
        heads(0)
        heads(1)
        tt(V("OH", 0, 256), IND(V("W", 0, 544), V("OFW", 0, 16)), V("K1", 0, 256), O.is_equal)
        mm2(V("PU", 0, 32), [(V("ID16"), V("CB"))], wraps("SD", "OH"))
        tt(V("CG", 0, 512), IND(V("YW"), V("OFC")), V("OH", 0, 512), O.mult)
        mm(V("PN", 0, 32), wraps("S32", "CG"))
        cp(V("OFN"), V("PU", 0, 32))
        order = [T.cores.index(d) for d in hop] + [me]
        blk = {o: ("SND", r * SL + o * 144) for o in order}
        blk[me] = ("A", (r + 1) * SL + me * 144)
        for k, o in enumerate(order):
            out, v = V(blk[o][0], blk[o][1], blk[o][1] + 128), IND(V("CH"), V("OFN", o * 8, o * 8 + 8))
            if k == 1:
                cp(out, v)
            else:
                act(out, v, F.Copy)
        pre(r)
        split([(o, (blk[o][0], blk[o][1] + 128)) for o in order[:3]])
        send(r, "a", "SND", ("A", (r + 1) * SL + me * 144), {d: blk[T.cores.index(d)][1] for d in hop}, 144)
        split([(me, (blk[me][0], blk[me][1] + 128))])
        arrive(r, "a", "A", (r + 1) * SL, 144, 144)
        if not r:
            consts3()

    for r in range(NR):
        rnd(r)
    level_a(NR - 1)

    for l in range(3):
        ts(V("OG3", l * 40, l * 40 + 40), V("CL"), C(9 + l), O.add)
    ts(w_(0, 3), HI, -1023.0, O.add, 1.0 / 32, O.mult)
    for l in range(3):
        cp(V("FF", l * 128, l * 128 + 128), IND(V("A"), V("OG3", l * 40 + 32, l * 40 + 40)))
    for k in range(12):
        l, q = k // 4, k % 4
        act(V("S3", k * 256, k * 256 + 128), IND(V("A"), V("OG3", l * 40 + q * 8, l * 40 + q * 8 + 8)), F.Copy)
    for l in range(3):
        a, b = l * 32, l * 32 + 32
        tt(V("F3", a, b), V("FF", l * 128, l * 128 + 32), V("FF", l * 128 + 64, l * 128 + 96), O.add)
    for l in range(3):
        a, b = l * 32, l * 32 + 32
        ts(V("KP3", a, b), V("F3", a, b), w_(l), O.is_lt)
    scan(V("R3"), V("RM"), V("KP3"), O.mult, O.add)
    mm(V("PEA", 0, 96), [(V("BLK"), V("R3"))])
    mm(V("PC0", 0, 96), [(V("BLK"), V("R3")), (V("NUT"), V("KP3"))])
    tt(V("EM"), V("PEA", 0, 96), V("DM3"), O.mult)
    for k in range(12):
        red(V("EA", k, k + 1), V("EM", k * 8, k * 8 + 8), O.add)
    ts(V("EA"), V("EA"), V("LC", 5, 6), O.add)
    for k in range(12):
        ts(V("IA", k * 128, k * 128 + 128), V("K", 0, 128), V("EA", k, k + 1), O.is_ge)
    mm2(V("PL", 0, 96), [(V("ID"), V("B8C"))], wraps("S1", "IA", 1536))
    tt(V("W3"), V("PC0", 0, 96), V("KP3"), O.mult)
    level_b()
    cp(V("YT", 0, 3), LO)
    cp(V("YT", 3, 6), HI)
    tt(w_(60), C(19), C(19), O.add)
    tt(V("YT", 6, 7), w_(60), C(18), O.add)
    cp(V("YT", 7, 8), U)
    mm(V("PX", 0, 8, P=8), [(V("G8F"), V("YT"))])
    cp(V("OF3"), V("PL", 0, 96))
    tt(V("AB"), V("PL", 0, 96), V("B8C"), O.subtract)
    for l in range(3):
        a, b = l * 512, l * 512 + 512
        tt(V("OH", a, b), IND(V("W3"), V("OF3", l * 32, l * 32 + 32)), V("K1"), O.is_equal)
    mm2(V("PU", 0, 96), [(V("ID16"), V("AB")), (V("ID"), V("B256"))], wraps("SE", "OH", 1536))
    cp(V("YT8", P=8), V("PX", 0, 8, P=8))
    dma("Y", EXT(T.yt[:, :]), V("YT8", P=8), "o0")

    def costs(l):
        a, b = l * 512, l * 512 + 512
        tt(V("CG", a, b), IND(V("F3"), V("OF3", l * 32, l * 32 + 32)), V("OH", a, b), O.mult)
        p = ("PC0", "PC1", "PEB")[l]
        mm(V(p, 0, 512, P=8), [(V("G8"), V("CG", a, b))])

    costs(0)
    cp(V("OP3"), V("PU", 0, 96))
    for l in range(3):
        a, b = l * 512, l * 512 + 512
        act(V("YL", a, b), IND(V("S3"), V("OP3", l * 32, l * 32 + 32)), F.Copy)
        dma("Y", EXT(T.yl[:, a:b]), V("YL", a, b), "o%d" % (1 + l))
    costs(1)
    costs(2)
    for l in range(3):
        a, b = l * 512, l * 512 + 512
        ts(V("YF", a, b, P=8), V(("PC0", "PC1", "PEB")[l], 0, 512, P=8), 1023.0, O.add)
    dma("S", EXT(T.yf[:, :]), V("YF", P=8), "o4")
    for k in range(4):
        g.sync.wait_ge(T.sem["o%d" % k], 16)
    for k in range(9):
        g.sync.wait_ge(T.sem["l%d" % k], 16)
    g.scalar.wait_ge(T.sem.o4, 16)
    for e in ("V", "S", "T", "G"):
        g.wait_ge(T.sem["s" + e], count[e])
    g.wait_ge(T.sem.ls, count["ls"])
